import numpy as np
import ml_dtypes


def mxq(x, axis, fmt="e4m3"):
    dtype, down = {"e4m3": (ml_dtypes.float8_e4m3fn, 7), "e5m2": (ml_dtypes.float8_e5m2, 14)}[fmt]
    v = np.moveaxis(np.asarray(x, np.float32).astype(ml_dtypes.bfloat16).astype(np.float64), axis, -1)
    blocks = v.reshape(v.shape[:-1] + (-1, 32))
    amax = np.abs(blocks).max(-1, keepdims=True)
    byte = np.maximum(np.where(amax > 0, np.frexp(amax)[1] - 1 + 127, 0) - down, 1)
    scale = np.exp2(byte - 127.0)
    codes = (blocks / scale).astype(np.float32).astype(dtype).astype(np.float64)
    return np.moveaxis((codes * scale).reshape(v.shape), -1, axis)


WIDE = False


def mx_kscale(k):
    if not WIDE:
        return np.ones(k)
    levels = np.array([10, -10, 5, -5, 0])
    if k % 512:
        return np.exp2(np.random.permutation(np.resize(levels, k // 32))).repeat(32)
    a = np.empty((k // 512, 16))
    for p in range(k // 512):
        a[p, :8] = np.random.permutation(np.resize(levels, 8))
        for g in range(8):
            far = levels[np.abs(levels - a[p, g]) >= 10]
            a[p, g + 8] = far[np.random.randint(len(far))]
    return np.exp2(a.ravel()).repeat(32)


def f64(x):
    return np.asarray(x).astype(np.float64)


def striped(idx):
    return np.tile(idx.reshape(-1, 16).T, (8, 1)).astype(np.uint16)


def unstriped(offs):
    return offs[:16].T.reshape(-1).astype(np.int64)


E2M1 = np.array([0.0, 0.5, 1.0, 1.5, 2.0, 3.0, 4.0, 6.0, -0.0, -0.5, -1.0, -1.5, -2.0, -3.0, -4.0, -6.0])


def pack_weight(w, fmt):
    k, n = w.shape
    w = f64(np.asarray(w, np.float32).astype(ml_dtypes.bfloat16)).reshape(k // 32, 32, n)
    amax = np.abs(w).max(1)
    if fmt == "e4m3":
        byte = np.frexp(amax)[1] - 1 + 127 - 7
    else:
        mant, ex = np.frexp(amax / 6.0)
        byte = np.where(mant > 0.5, ex, ex - 1) + 127
    byte = np.clip(np.where(amax > 0, byte, 1), 1, 254)
    scaled = (w * np.exp2(127.0 - byte)[:, None, :]).reshape(k, n).astype(np.float32)
    by_word = np.ascontiguousarray(scaled.reshape(k // 512, 128, 4, n).transpose(0, 1, 3, 2))
    if fmt == "e4m3":
        words = by_word.astype(ml_dtypes.float8_e4m3fn).view(np.uint8)
    else:
        c = by_word.astype(ml_dtypes.float4_e2m1fn).view(np.uint8) & 0xF
        words = (c[..., 0::2] | (c[..., 1::2] << 4)).reshape(k // 512, 128, 2 * n)
    return np.ascontiguousarray(words), np.ascontiguousarray(byte.astype(np.uint8).reshape(k // 512, 16, n))


def unpack_weight(words, scales, fmt):
    g, _, n = scales.shape
    words = np.ascontiguousarray(words).reshape(g, 128, n, -1)
    if fmt == "e4m3":
        vals = words.view(ml_dtypes.float8_e4m3fn).astype(np.float64)
    else:
        nib = np.empty((g, 128, n, 4), np.uint8)
        nib[..., 0::2] = words & 0xF
        nib[..., 1::2] = words >> 4
        vals = E2M1[nib]
    vals = vals * np.repeat(np.exp2(scales.astype(np.float64) - 127.0), 8, axis=1)[..., None]
    return vals.transpose(0, 1, 3, 2).reshape(g * 512, n)


K, T, E, C, N = 512, 768, 6, 128, 1024
M = 512


def by_expert(wq, xq):
    return np.concatenate([wq[e].T @ xq[:, e * C:(e + 1) * C] for e in range(E)], axis=1)


def setup_inputs():
    n = np.random.standard_normal
    s = mx_kscale(K)[:, None]
    v = mx_kscale(N)
    w = [pack_weight(m, "e2m1") for m in n((E, K, N)) / np.sqrt(K) / s[None] * v[None, None, :]]
    return {
        "xT": (n((K, T)) * s).astype(np.float32),
        "w_words": np.stack([m[0] for m in w]),
        "w_scales": np.stack([m[1] for m in w]),
        "wp": (n((N, M)) / np.sqrt(N) / v[:, None]).astype(np.float32),
        "gate": np.tile(np.random.uniform(0.2, 1.0, E * C), (N, 1)).astype(np.float32),
        "offs": striped(np.random.permutation(T)[:E * C]),
    }


def reference(xT, w_words, w_scales, wp, gate, offs):
    idx = unstriped(offs)
    w = np.stack([unpack_weight(w_words[e], w_scales[e], "e2m1") for e in range(E)])
    xq = mxq(f64(xT)[:, idx], 0, "e4m3")
    y = by_expert(w, xq)
    c = np.zeros((N, T))
    c[:, idx] = f64(gate) * y
    return mxq(f64(wp), 0, "e4m3").T @ mxq(c, 0, "e4m3")

@@ -1,0 +1,268 @@
+from contextlib import ExitStack
+
+import concourse.mybir as mybir
+from concourse.masks import make_identity
+
+K, T, E, C, N, M = 512, 768, 6, 128, 1024, 512
+P = 128
+PACK = 4
+PASSES = N // 512
+F_TILES = M // P
+
+FLOPS = 2 * K * N * E * C + 2 * N * M * T
+BYTES = 4 * K * T + E * K * N // 2 + E * (K // 32) * N + 4 * N * M + 4 * E * C + 2 * E * C + 4 * M * T
+
+F32 = mybir.dt.float32
+BF16 = mybir.dt.bfloat16
+I32 = mybir.dt.int32
+U32 = mybir.dt.uint32
+U16 = mybir.dt.uint16
+U8 = mybir.dt.uint8
+FP8X4 = mybir.dt.float8_e4m3fn_x4
+FP4X4 = mybir.dt.float4_e2m1fn_x4
+COPY = mybir.ActivationFunctionType.Copy
+MULT = mybir.AluOpType.mult
+
+
+def interleave(copy, dst, src, a, b):
+    copy(
+        out=dst[:, PACK * a : PACK * b].rearrange("p (c i j) -> p c j i", i=4, j=PACK),
+        in_=src[:, :, a:b].rearrange("p j (c i) -> p c j i", i=4),
+    )
+
+
+def tile_moe_nxt_lin_none_kernel(tc, xT, w_words, w_scales, wp, gate, offs, out):
+    nc = tc.nc
+    with ExitStack() as ctx:
+        keep = ctx.enter_context(tc.tile_pool(name="keep", bufs=1))
+        psum_y = ctx.enter_context(tc.psum_pool(name="psum_y", bufs=4))
+        psum_t = ctx.enter_context(tc.psum_pool(name="psum_t", bufs=2))
+        psum_o = ctx.enter_context(tc.psum_pool(name="psum_o", bufs=2))
+
+        offsets = keep.tile([P, E * C // 16], U16, name="offsets")
+        gate_cols = keep.tile([P, E], F32, name="gate_cols")
+        gate_rows = keep.tile([P, P], F32, name="gate_rows")
+        ident = keep.tile([P, P], F32, name="ident")
+        x_codes = keep.tile([P, T], U32, name="x_codes", align_bytes=64)
+        x_scales = keep.tile([P, T], U8, name="x_scales", align_bytes=64)
+        s_codes = keep.tile([P, E * C], U32, name="s_codes", align_bytes=64)
+        s_scales = keep.tile([P, E * C], U8, name="s_scales", align_bytes=64)
+        w_codes = keep.tile([P, E, 2 * N], U8, name="w_codes", align_bytes=64)
+        w_planes = keep.tile([P, E, N], U8, name="w_planes", align_bytes=64)
+
+        nc.vector.memset(w_planes[:].rearrange("p e n -> p (e n)").bitcast(I32), 0)
+        nc.gpsimd.memset(x_scales[:], 0)
+        nc.gpsimd.memset(gate_rows[:], 0.0)
+        make_identity(nc, ident[:])
+
+        x_view = xT.rearrange("(p j) t -> p j t", j=PACK)
+        x_cuts = ((0, 256), (256, 512), (512, T))
+        x_raw = []
+        for a, b in x_cuts:
+            raw = keep.tile([P, PACK, b - a], F32, name=f"x_raw{a}")
+            nc.sync.dma_start(out=raw[:], in_=x_view[:, :, a:b])
+            x_raw.append(raw)
+        nc.sync.dma_start(offsets[:], offs)
+        nc.sync.dma_start(out=gate_rows[0:E, :], in_=gate[0:1, :].rearrange("o (e p) -> (o e) p", p=P))
+
+        def load_w(a, b):
+            nc.sync.dma_start(out=w_codes[:, a:b, :].bitcast(I32), in_=w_words[a:b, 0].rearrange("e p n -> p e n").bitcast(I32))
+
+        wp_view = wp.rearrange("(g p j) f -> g p j f", p=P, j=PACK)
+        wp_raw = {}
+
+        def load_wp(half, g):
+            raw = keep.tile([P, PACK, M // 2], F32, name=f"wp_raw{half}{g}")
+            nc.sync.dma_start(out=raw[:], in_=wp_view[g, :, :, half * (M // 2) : (half + 1) * (M // 2)])
+            wp_raw[half, g] = raw
+
+        load_wp(0, 0)
+        load_w(0, 1)
+        scale_rows = w_scales.bitcast(I32).rearrange("e a (q r) n -> r q (e a) n", r=4)
+        for r in range(4):
+            nc.sync.dma_start(out=w_planes[r:P:32, :, :].bitcast(I32), in_=scale_rows[r])
+        load_wp(0, 1)
+        load_w(1, 3)
+        load_wp(1, 0)
+        load_wp(1, 1)
+        load_w(3, E)
+
+        x_group = keep.tile([P, PACK * T], BF16, name="x_group", align_bytes=64)
+        for (a, b), raw in zip(x_cuts, x_raw):
+            width = b - a
+            dst = x_group[:, PACK * a : PACK * b]
+            cut = 96
+            interleave(nc.scalar.copy, dst, raw, 0, cut)
+            interleave(nc.vector.tensor_copy, dst, raw, cut, width)
+            nc.vector.quantize_mx(out=x_codes[:, a:b].bitcast(FP8X4), scales=x_scales[:, a:b], in_=dst)
+
+        def gather(a, b):
+            at = offsets[:, a * C // 16 : b * C // 16]
+            nc.vector.tensor_copy(s_codes[:, a * C : b * C], x_codes[:].indirect(at))
+            nc.vector.tensor_copy(s_scales[:, a * C : b * C], x_scales[:].indirect(at))
+
+        def gate_times(e, g, y, c_rows, on_vector):
+            dst = c_rows[:, 512 * g : 512 * (g + 1)].rearrange("s (u p i) -> s u p i", u=2, i=2)
+            src = y[:].rearrange("s (p u i) -> s u p i", u=2, i=2)
+            if on_vector:
+                nc.vector.tensor_scalar(dst, src, gate_cols[:, e : e + 1], None, MULT)
+            else:
+                nc.scalar.activation(out=dst, in_=src, func=COPY, scale=gate_cols[:, e : e + 1])
+
+        ys = {}
+
+        def product(e):
+            ys[e] = []
+            for g in range(PASSES):
+                y = psum_y.tile([P, 512], F32, name="y")
+                nc.tensor.matmul_mx(
+                    out=y[:],
+                    lhsT=s_codes[:, e * C : (e + 1) * C].bitcast(FP8X4),
+                    lhsT_scale=s_scales[:, e * C : (e + 1) * C],
+                    rhs=w_codes[:, e, 1024 * g : 1024 * (g + 1)].bitcast(FP4X4),
+                    rhs_scale=w_planes[:, e, 512 * g : 512 * (g + 1)],
+                    start=True,
+                    stop=True,
+                )
+                ys[e].append(y)
+
+        groups = {}
+
+        rows, turned_of, groups, c_quant, sums, landed = {}, {}, {}, {}, {}, {}
+
+        def gated_rows(e, g, on_vector=False):
+            if g == 0:
+                rows[e] = keep.tile([P, N], BF16, name=f"c_rows{e}", tag=f"swap{e}", align_bytes=64)
+            gate_times(e, g, ys[e][g], rows[e], on_vector)
+
+        def turn(e):
+            turned = psum_t.tile([P, PASSES, 2, C], F32, name="turned")
+            words = rows[e][:].bitcast(F32)
+            for g in range(PASSES):
+                for u in range(2):
+                    at = 256 * g + 128 * u
+                    nc.tensor.transpose(turned[:, g, u, :], words[:, at : at + 128], ident[:])
+            turned_of[e] = turned
+
+        def group_c(unit, e):
+            width = len(unit) * C
+            if e == unit[0]:
+                groups[unit] = keep.tile([P, PASSES, width, PACK], BF16, name=f"c_group{e}", align_bytes=64)
+            words = groups[unit][:].rearrange("p g s j -> p (g s j)").bitcast(F32).rearrange("p (g s u) -> p g s u", g=PASSES, u=2)
+            at = (e - unit[0]) * C
+            nc.scalar.copy(out=words[:, :, at : at + C, :], in_=turned_of[e][:].rearrange("p g u s -> p g s u"))
+
+        def quantise_c(unit):
+            width = len(unit) * C
+            codes = keep.tile([P, PASSES, width], U32, name=f"c_codes{unit[0]}", align_bytes=64)
+            scales = keep.tile([P, PASSES, width], U8, name=f"c_scales{unit[0]}", align_bytes=64)
+            nc.vector.quantize_mx(
+                out=codes[:].rearrange("p g s -> p (g s)").bitcast(FP8X4),
+                scales=scales[:].rearrange("p g s -> p (g s)"),
+                in_=groups[unit][:].rearrange("p g s j -> p (g s j)"),
+            )
+            c_quant[unit] = (codes, scales)
+
+        half_width = M // 2
+        wp_codes, wp_scales, wp_group = [], [], []
+        for half in range(2):
+            wp_group.append(keep.tile([P, PASSES * half_width * PACK], BF16, name=f"wp_group{half}", align_bytes=64))
+            wp_codes.append(keep.tile([P, PASSES, half_width], U32, name=f"wp_codes{half}", align_bytes=64))
+            wp_scales.append(keep.tile([P, PASSES, half_width], U8, name=f"wp_scales{half}", align_bytes=64))
+
+        def pool_copy(out, in_):
+            nc.gpsimd.tensor_scalar(out, in_, 1.0, 0.0, MULT, mybir.AluOpType.add)
+
+        def group_wp(half, g, copy):
+            dst = wp_group[half][:, PACK * half_width * g : PACK * half_width * (g + 1)]
+            interleave(copy, dst, wp_raw[half, g], 0, half_width)
+
+        def quantise_wp(half):
+            nc.vector.quantize_mx(
+                out=wp_codes[half][:].rearrange("p g f -> p (g f)").bitcast(FP8X4),
+                scales=wp_scales[half][:].rearrange("p g f -> p (g f)"),
+                in_=wp_group[half][:],
+            )
+
+        windows = [keep.tile([P, T], F32, name=f"window{f}") for f in range(F_TILES)]
+
+        def next_projection(unit, f_tiles):
+            width = len(unit) * C
+            o = psum_o.tile([P, 512], F32, name="o")
+            codes, scales = c_quant[unit]
+            for i, f in enumerate(f_tiles):
+                half, at = f // 2, (f % 2) * P
+                for g in range(PASSES):
+                    nc.tensor.matmul_mx(
+                        out=o[:, i * width : (i + 1) * width],
+                        lhsT=wp_codes[half][:, g, at : at + P].bitcast(FP8X4),
+                        lhsT_scale=wp_scales[half][:, g, at : at + P],
+                        rhs=codes[:, g, :].bitcast(FP8X4),
+                        rhs_scale=scales[:, g, :],
+                        start=(g == 0),
+                        stop=(g == PASSES - 1),
+                    )
+            sums[unit, f_tiles] = o
+
+        def land(unit, f_tiles, after=None):
+            width = len(unit) * C
+            label = f"landed{unit[0]}{f_tiles[0]}"
+            tag = f"swap{after[-1]}" if after else label
+            tile = keep.tile([P, len(f_tiles), width], F32, name=label, tag=tag, align_bytes=64)
+            nc.scalar.copy(
+                out=tile[:].rearrange("p f s -> p (f s)"), in_=sums[unit, f_tiles][:, : len(f_tiles) * width]
+            )
+            for i, f in enumerate(f_tiles):
+                landed[unit, f] = tile[:, i, :]
+
+        def scatter(unit, f):
+            a, b = unit[0], unit[-1] + 1
+            nc.vector.tensor_copy(windows[f][:].indirect(offsets[:, a * C // 16 : b * C // 16]), landed[unit, f])
+
+        low, high = (0, 1), (2, 3)
+        units = ((0,), (1,), (2,), (3, 4), (5,))
+
+        gather(0, 1)
+        turned = psum_t.tile([P, PASSES, 2, C], F32, name="turned")
+        nc.tensor.transpose(turned[:, 0, 0, :], gate_rows[:], ident[:])
+        nc.vector.tensor_copy(out=gate_cols[:], in_=turned[:, 0, 0, 0:E])
+        product(0)
+        group_wp(0, 0, nc.scalar.copy)
+        gated_rows(0, 0)
+        gated_rows(0, 1, True)
+        turn(0)
+        group_c(units[0], 0)
+        group_wp(0, 1, nc.vector.tensor_copy)
+        quantise_c(units[0])
+        quantise_wp(0)
+        next_projection(units[0], low)
+        land(units[0], low)
+        gather(1, 3)
+        group_wp(1, 0, pool_copy)
+        group_wp(1, 1, nc.vector.tensor_copy)
+        quantise_wp(1)
+        next_projection(units[0], high)
+        land(units[0], high)
+        for i in range(1, len(units)):
+            unit = units[i]
+            for e in unit:
+                if e == 3:
+                    gather(3, E)
+                product(e)
+                gated_rows(e, 0)
+                gated_rows(e, 1)
+                turn(e)
+                group_c(unit, e)
+            quantise_c(unit)
+            if i > 1:
+                land(units[i - 1], high, after=unit)
+            next_projection(unit, low)
+            land(unit, low)
+            next_projection(unit, high)
+        land(units[-1], high)
+        for unit in units[:-1]:
+            for f in low + high:
+                scatter(unit, f)
+        for f in low + high:
+            scatter(units[-1], f)
+            nc.sync.dma_start(out=out[f * P : (f + 1) * P, :], in_=windows[f][:])

@@ -36,23 +36,21 @@ def tile_moe_nxt_lin_none_kernel(tc, xT, w_words, w_scales, wp, gate, offs, out)
     with ExitStack() as ctx:
         keep = ctx.enter_context(tc.tile_pool(name="keep", bufs=1))
         psum_y = ctx.enter_context(tc.psum_pool(name="psum_y", bufs=4))
-        psum_t = ctx.enter_context(tc.psum_pool(name="psum_t", bufs=2))
-        psum_o = ctx.enter_context(tc.psum_pool(name="psum_o", bufs=2))
+        psum = ctx.enter_context(tc.psum_pool(name="psum", bufs=1))
 
         offsets = keep.tile([P, E * C // 16], U16, name="offsets")
-        gate_cols = keep.tile([P, E], F32, name="gate_cols")
-        gate_rows = keep.tile([P, P], F32, name="gate_rows")
+        gate_cols = keep.tile([P, 3, 2], F32, name="gate_cols")
+        gate_rows = keep.tile([P, 3 * P], F32, name="gate_rows")
         ident = keep.tile([P, P], F32, name="ident")
         x_codes = keep.tile([P, T], U32, name="x_codes", align_bytes=64)
         x_scales = keep.tile([P, T], U8, name="x_scales", align_bytes=64)
-        s_codes = keep.tile([P, E * C], U32, name="s_codes", align_bytes=64)
-        s_scales = keep.tile([P, E * C], U8, name="s_scales", align_bytes=64)
-        w_codes = keep.tile([P, E, 2 * N], U8, name="w_codes", align_bytes=64)
-        w_planes = keep.tile([P, E, N], U8, name="w_planes", align_bytes=64)
+        w_groups = ((0, 3), (3, E))
+        w_planes = [keep.tile([P, b - a, N], U8, name=f"w_planes{a}", align_bytes=64) for a, b in w_groups]
 
-        nc.vector.memset(w_planes[:].rearrange("p e n -> p (e n)").bitcast(I32), 0)
-        nc.gpsimd.memset(x_scales[:], 0)
         nc.gpsimd.memset(gate_rows[:], 0.0)
+        for planes in w_planes:
+            nc.vector.memset(planes[:].rearrange("p e n -> p (e n)").bitcast(I32), 0)
+        nc.gpsimd.memset(x_scales[:], 0)
         make_identity(nc, ident[:])
 
         x_view = xT.rearrange("(p j) t -> p j t", j=PACK)
@@ -62,30 +60,49 @@ def tile_moe_nxt_lin_none_kernel(tc, xT, w_words, w_scales, wp, gate, offs, out)
             raw = keep.tile([P, PACK, b - a], F32, name=f"x_raw{a}")
             nc.sync.dma_start(out=raw[:], in_=x_view[:, :, a:b])
             x_raw.append(raw)
-        nc.sync.dma_start(offsets[:], offs)
-        nc.sync.dma_start(out=gate_rows[0:E, :], in_=gate[0:1, :].rearrange("o (e p) -> (o e) p", p=P))
+            if a == 0:
+                nc.sync.dma_start(offsets[:], offs)
+                nc.sync.dma_start(out=gate_rows[0:2, :], in_=gate[0:1, :].rearrange("o (r s) -> (o r) s", r=2))
+
+        w_codes = {}
 
         def load_w(a, b):
-            nc.sync.dma_start(out=w_codes[:, a:b, :].bitcast(I32), in_=w_words[a:b, 0].rearrange("e p n -> p e n").bitcast(I32))
+            words = keep.tile([P, b - a, 2 * N], U8, name=f"w_codes{a}", align_bytes=64)
+            nc.sync.dma_start(out=words[:].bitcast(I32), in_=w_words[a:b, 0].rearrange("e p n -> p e n").bitcast(I32))
+            for e in range(a, b):
+                w_codes[e] = words[:, e - a, :]
+
+        scale_rows = w_scales.bitcast(I32).rearrange("e a (q r) n -> r q (e a) n", r=4)
+
+        def load_scales(i):
+            a, b = w_groups[i]
+            for r in range(4):
+                nc.sync.dma_start(out=w_planes[i][r:P:32, :, :].bitcast(I32), in_=scale_rows[r, :, a:b, :])
 
         wp_view = wp.rearrange("(g p j) f -> g p j f", p=P, j=PACK)
+        half_width = M // 2
         wp_raw = {}
 
         def load_wp(half, g):
-            raw = keep.tile([P, PACK, M // 2], F32, name=f"wp_raw{half}{g}")
-            nc.sync.dma_start(out=raw[:], in_=wp_view[g, :, :, half * (M // 2) : (half + 1) * (M // 2)])
+            raw = keep.tile([P, PACK, half_width], F32, name=f"wp_raw{half}{g}", tag=f"wp_raw{half}{g}", align_bytes=64)
+            nc.sync.dma_start(out=raw[:], in_=wp_view[g, :, :, half * half_width : (half + 1) * half_width])
             wp_raw[half, g] = raw
 
+        load_scales(0)
         load_wp(0, 0)
         load_w(0, 1)
-        scale_rows = w_scales.bitcast(I32).rearrange("e a (q r) n -> r q (e a) n", r=4)
-        for r in range(4):
-            nc.sync.dma_start(out=w_planes[r:P:32, :, :].bitcast(I32), in_=scale_rows[r])
+        load_w(1, 2)
         load_wp(0, 1)
-        load_w(1, 3)
+        load_w(2, 3)
         load_wp(1, 0)
         load_wp(1, 1)
+        load_scales(1)
         load_w(3, E)
+
+        gate_turned = psum.tile([P, PASSES * 2, C], F32, name="gate_turned", tag="bank1")
+        for c in range(3):
+            nc.tensor.transpose(gate_turned[:, c, :], gate_rows[:, c * P : (c + 1) * P], ident[:])
+        nc.scalar.copy(out=gate_cols[:], in_=gate_turned[:, 0:3, 0:2])
 
         x_group = keep.tile([P, PACK * T], BF16, name="x_group", align_bytes=64)
         for (a, b), raw in zip(x_cuts, x_raw):
@@ -96,61 +113,52 @@ def tile_moe_nxt_lin_none_kernel(tc, xT, w_words, w_scales, wp, gate, offs, out)
             interleave(nc.vector.tensor_copy, dst, raw, cut, width)
             nc.vector.quantize_mx(out=x_codes[:, a:b].bitcast(FP8X4), scales=x_scales[:, a:b], in_=dst)
 
-        def gather(a, b):
+        s_codes, s_scales = {}, {}
+
+        def gather(a, b, tag=None):
             at = offsets[:, a * C // 16 : b * C // 16]
-            nc.vector.tensor_copy(s_codes[:, a * C : b * C], x_codes[:].indirect(at))
-            nc.vector.tensor_copy(s_scales[:, a * C : b * C], x_scales[:].indirect(at))
+            codes = keep.tile([P, (b - a) * C], U32, name=f"s_codes{a}", tag=tag or f"s_codes{a}", align_bytes=64)
+            scales = keep.tile([P, (b - a) * C], U8, name=f"s_scales{a}", align_bytes=64)
+            nc.vector.tensor_copy(codes[:], x_codes[:].indirect(at))
+            nc.vector.tensor_copy(scales[:], x_scales[:].indirect(at))
+            for e in range(a, b):
+                s_codes[e] = codes[:, (e - a) * C : (e - a + 1) * C]
+                s_scales[e] = scales[:, (e - a) * C : (e - a + 1) * C]
 
-        def gate_times(e, g, y, c_rows, on_vector):
-            dst = c_rows[:, 512 * g : 512 * (g + 1)].rearrange("s (u p i) -> s u p i", u=2, i=2)
-            src = y[:].rearrange("s (p u i) -> s u p i", u=2, i=2)
-            if on_vector:
-                nc.vector.tensor_scalar(dst, src, gate_cols[:, e : e + 1], None, MULT)
-            else:
-                nc.scalar.activation(out=dst, in_=src, func=COPY, scale=gate_cols[:, e : e + 1])
+        rows, turned_of, groups, c_quant, sums, landed = {}, {}, {}, {}, {}, {}
 
-        ys = {}
-
-        def product(e):
-            ys[e] = []
+        def gated_product(e):
+            rows[e] = keep.tile([P, N], BF16, name=f"c_rows{e}", tag=f"rows{e}", align_bytes=64)
+            i = 0 if e < w_groups[0][1] else 1
             for g in range(PASSES):
                 y = psum_y.tile([P, 512], F32, name="y")
                 nc.tensor.matmul_mx(
                     out=y[:],
-                    lhsT=s_codes[:, e * C : (e + 1) * C].bitcast(FP8X4),
-                    lhsT_scale=s_scales[:, e * C : (e + 1) * C],
-                    rhs=w_codes[:, e, 1024 * g : 1024 * (g + 1)].bitcast(FP4X4),
-                    rhs_scale=w_planes[:, e, 512 * g : 512 * (g + 1)],
+                    lhsT=s_codes[e].bitcast(FP8X4),
+                    lhsT_scale=s_scales[e],
+                    rhs=w_codes[e][:, 1024 * g : 1024 * (g + 1)].bitcast(FP4X4),
+                    rhs_scale=w_planes[i][:, e - w_groups[i][0], 512 * g : 512 * (g + 1)],
                     start=True,
                     stop=True,
                 )
-                ys[e].append(y)
+                nc.scalar.activation(
+                    out=rows[e][:, 512 * g : 512 * (g + 1)].rearrange("s (u p i) -> s u p i", u=2, i=2),
+                    in_=y[:].rearrange("s (p u i) -> s u p i", u=2, i=2),
+                    func=COPY,
+                    scale=gate_cols[:, e % 3, e // 3 : e // 3 + 1],
+                )
 
-        groups = {}
-
-        rows, turned_of, groups, c_quant, sums, landed = {}, {}, {}, {}, {}, {}
-
-        def gated_rows(e, g, on_vector=False):
-            if g == 0:
-                rows[e] = keep.tile([P, N], BF16, name=f"c_rows{e}", tag=f"swap{e}", align_bytes=64)
-            gate_times(e, g, ys[e][g], rows[e], on_vector)
-
-        def turn(e):
-            turned = psum_t.tile([P, PASSES, 2, C], F32, name="turned")
+        def turn(unit, e, bank):
+            turned = psum.tile([P, PASSES * 2, C], F32, name=f"turned{e}", tag=f"bank{bank}")
             words = rows[e][:].bitcast(F32)
-            for g in range(PASSES):
-                for u in range(2):
-                    at = 256 * g + 128 * u
-                    nc.tensor.transpose(turned[:, g, u, :], words[:, at : at + 128], ident[:])
-            turned_of[e] = turned
-
-        def group_c(unit, e):
+            for h in range(PASSES * 2):
+                nc.tensor.transpose(turned[:, h, :], words[:, C * h : C * (h + 1)], ident[:])
             width = len(unit) * C
             if e == unit[0]:
-                groups[unit] = keep.tile([P, PASSES, width, PACK], BF16, name=f"c_group{e}", align_bytes=64)
-            words = groups[unit][:].rearrange("p g s j -> p (g s j)").bitcast(F32).rearrange("p (g s u) -> p g s u", g=PASSES, u=2)
+                groups[unit] = keep.tile([P, PASSES, width, PACK], BF16, name=f"c_group{e}", tag=f"group{e}", align_bytes=64)
+            pairs = groups[unit][:].rearrange("p g s j -> p (g s j)").bitcast(F32).rearrange("p (g s u) -> p g s u", g=PASSES, u=2)
             at = (e - unit[0]) * C
-            nc.scalar.copy(out=words[:, :, at : at + C, :], in_=turned_of[e][:].rearrange("p g u s -> p g s u"))
+            nc.scalar.copy(out=pairs[:, :, at : at + C, :], in_=turned[:].rearrange("p (g u) s -> p g s u", u=2))
 
         def quantise_c(unit):
             width = len(unit) * C
@@ -163,106 +171,93 @@ def tile_moe_nxt_lin_none_kernel(tc, xT, w_words, w_scales, wp, gate, offs, out)
             )
             c_quant[unit] = (codes, scales)
 
-        half_width = M // 2
-        wp_codes, wp_scales, wp_group = [], [], []
-        for half in range(2):
-            wp_group.append(keep.tile([P, PASSES * half_width * PACK], BF16, name=f"wp_group{half}", align_bytes=64))
-            wp_codes.append(keep.tile([P, PASSES, half_width], U32, name=f"wp_codes{half}", align_bytes=64))
-            wp_scales.append(keep.tile([P, PASSES, half_width], U8, name=f"wp_scales{half}", align_bytes=64))
+        wp_group, wp_quant = {}, {}
 
         def pool_copy(out, in_):
             nc.gpsimd.tensor_scalar(out, in_, 1.0, 0.0, MULT, mybir.AluOpType.add)
 
         def group_wp(half, g, copy):
-            dst = wp_group[half][:, PACK * half_width * g : PACK * half_width * (g + 1)]
-            interleave(copy, dst, wp_raw[half, g], 0, half_width)
+            if g == 0:
+                wp_group[half] = keep.tile([P, PASSES, half_width * PACK], BF16, name=f"wp_group{half}", tag=f"wp_group{half}", align_bytes=64)
+            interleave(copy, wp_group[half][:, g, :], wp_raw[half, g], 0, half_width)
 
-        def quantise_wp(half):
+        def quantise_wp(half, passes, tag=None):
+            label = f"wp_codes{half}{passes[0]}"
+            codes = keep.tile([P, len(passes), half_width], U32, name=label, tag=tag or label, align_bytes=64)
+            scales = keep.tile([P, len(passes), half_width], U8, name=f"wp_scales{half}{passes[0]}", align_bytes=64)
             nc.vector.quantize_mx(
-                out=wp_codes[half][:].rearrange("p g f -> p (g f)").bitcast(FP8X4),
-                scales=wp_scales[half][:].rearrange("p g f -> p (g f)"),
-                in_=wp_group[half][:],
+                out=codes[:].rearrange("p g f -> p (g f)").bitcast(FP8X4),
+                scales=scales[:].rearrange("p g f -> p (g f)"),
+                in_=wp_group[half][:, passes[0] : passes[-1] + 1, :].rearrange("p g f -> p (g f)"),
             )
+            for i, g in enumerate(passes):
+                wp_quant[half, g] = (codes[:, i, :], scales[:, i, :])
 
         windows = [keep.tile([P, T], F32, name=f"window{f}") for f in range(F_TILES)]
 
-        def next_projection(unit, f_tiles):
-            width = len(unit) * C
-            o = psum_o.tile([P, 512], F32, name="o")
-            codes, scales = c_quant[unit]
+        def project(units, f_tiles, bank, tag=None):
+            width = sum(len(unit) for unit in units) * C
+            o = psum.tile([P, 512], F32, name=f"o{units[0][0]}{f_tiles[0]}", tag=f"bank{bank}")
             for i, f in enumerate(f_tiles):
                 half, at = f // 2, (f % 2) * P
-                for g in range(PASSES):
-                    nc.tensor.matmul_mx(
-                        out=o[:, i * width : (i + 1) * width],
-                        lhsT=wp_codes[half][:, g, at : at + P].bitcast(FP8X4),
-                        lhsT_scale=wp_scales[half][:, g, at : at + P],
-                        rhs=codes[:, g, :].bitcast(FP8X4),
-                        rhs_scale=scales[:, g, :],
-                        start=(g == 0),
-                        stop=(g == PASSES - 1),
-                    )
-            sums[unit, f_tiles] = o
-
-        def land(unit, f_tiles, after=None):
-            width = len(unit) * C
-            label = f"landed{unit[0]}{f_tiles[0]}"
-            tag = f"swap{after[-1]}" if after else label
-            tile = keep.tile([P, len(f_tiles), width], F32, name=label, tag=tag, align_bytes=64)
-            nc.scalar.copy(
-                out=tile[:].rearrange("p f s -> p (f s)"), in_=sums[unit, f_tiles][:, : len(f_tiles) * width]
-            )
+                col = i * width
+                for unit in units:
+                    codes, scales = c_quant[unit]
+                    for g in range(PASSES):
+                        nc.tensor.matmul_mx(
+                            out=o[:, col : col + len(unit) * C],
+                            lhsT=wp_quant[half, g][0][:, at : at + P].bitcast(FP8X4),
+                            lhsT_scale=wp_quant[half, g][1][:, at : at + P],
+                            rhs=codes[:, g, :].bitcast(FP8X4),
+                            rhs_scale=scales[:, g, :],
+                            start=(g == 0),
+                            stop=(g == PASSES - 1),
+                        )
+                    col = col + len(unit) * C
+            label = f"landed{units[0][0]}{f_tiles[0]}"
+            landed = keep.tile([P, len(f_tiles), width], F32, name=label, tag=tag or label, align_bytes=64)
+            nc.scalar.copy(out=landed[:].rearrange("p f s -> p (f s)"), in_=o[:, : len(f_tiles) * width])
+            sums[units[0][0], f_tiles[0]] = landed
+            a, b = units[0][0], units[-1][-1] + 1
             for i, f in enumerate(f_tiles):
-                landed[unit, f] = tile[:, i, :]
-
-        def scatter(unit, f):
-            a, b = unit[0], unit[-1] + 1
-            nc.vector.tensor_copy(windows[f][:].indirect(offsets[:, a * C // 16 : b * C // 16]), landed[unit, f])
+                nc.vector.tensor_copy(windows[f][:].indirect(offsets[:, a * C // 16 : b * C // 16]), landed[:, i, :])
+                if b == E:
+                    nc.sync.dma_start(out=out[f * P : (f + 1) * P, :], in_=windows[f][:])
 
         low, high = (0, 1), (2, 3)
-        units = ((0,), (1,), (2,), (3, 4), (5,))
+        u0, u1, u2, u3, u45 = (0,), (1,), (2,), (3,), (4, 5)
 
         gather(0, 1)
-        turned = psum_t.tile([P, PASSES, 2, C], F32, name="turned")
-        nc.tensor.transpose(turned[:, 0, 0, :], gate_rows[:], ident[:])
-        nc.vector.tensor_copy(out=gate_cols[:], in_=turned[:, 0, 0, 0:E])
-        product(0)
         group_wp(0, 0, nc.scalar.copy)
-        gated_rows(0, 0)
-        gated_rows(0, 1, True)
-        turn(0)
-        group_c(units[0], 0)
-        group_wp(0, 1, nc.vector.tensor_copy)
-        quantise_c(units[0])
-        quantise_wp(0)
-        next_projection(units[0], low)
-        land(units[0], low)
+        gated_product(0)
         gather(1, 3)
+        turn(u0, 0, 0)
+        quantise_wp(0, (0,))
+        group_wp(0, 1, nc.vector.tensor_copy)
+        quantise_wp(0, (1,))
+        quantise_c(u0)
+        gated_product(1)
+        turn(u1, 1, 1)
+        quantise_c(u1)
+        gather(3, E, tag="group1")
+        gated_product(2)
+        turn(u2, 2, 0)
+        quantise_c(u2)
         group_wp(1, 0, pool_copy)
         group_wp(1, 1, nc.vector.tensor_copy)
-        quantise_wp(1)
-        next_projection(units[0], high)
-        land(units[0], high)
-        for i in range(1, len(units)):
-            unit = units[i]
-            for e in unit:
-                if e == 3:
-                    gather(3, E)
-                product(e)
-                gated_rows(e, 0)
-                gated_rows(e, 1)
-                turn(e)
-                group_c(unit, e)
-            quantise_c(unit)
-            if i > 1:
-                land(units[i - 1], high, after=unit)
-            next_projection(unit, low)
-            land(unit, low)
-            next_projection(unit, high)
-        land(units[-1], high)
-        for unit in units[:-1]:
-            for f in low + high:
-                scatter(unit, f)
-        for f in low + high:
-            scatter(units[-1], f)
-            nc.sync.dma_start(out=out[f * P : (f + 1) * P, :], in_=windows[f][:])
+        for g in range(PASSES):
+            quantise_wp(1, (g,))
+        project((u0,), low, 1)
+        project((u0,), high, 2)
+        project((u1,), low + high, 3, tag="rows2")
+        gated_product(3)
+        turn(u3, 3, 1)
+        quantise_c(u3)
+        project((u2,), low + high, 1)
+        for e in u45:
+            gated_product(e)
+            turn(u45, e, e - 2)
+        quantise_c(u45)
+        project((u3,), low + high, 3)
+        project((u45,), low, 0)
+        project((u45,), high, 1)

@@ -35,6 +35,7 @@ def tile_moe_nxt_lin_none_kernel(tc, xT, w_words, w_scales, wp, gate, offs, out)
     nc = tc.nc
     with ExitStack() as ctx:
         keep = ctx.enter_context(tc.tile_pool(name="keep", bufs=1))
+        shared = ctx.enter_context(tc.tile_pool(name="shared", bufs=1))
         psum_y = ctx.enter_context(tc.psum_pool(name="psum_y", bufs=4))
         psum = ctx.enter_context(tc.psum_pool(name="psum", bufs=1))
 
@@ -91,15 +92,15 @@ def tile_moe_nxt_lin_none_kernel(tc, xT, w_words, w_scales, wp, gate, offs, out)
         load_scales(0)
         load_wp(0, 0)
         load_w(0, 1)
-        load_w(1, 2)
         load_wp(0, 1)
+        load_w(1, 2)
         load_w(2, 3)
         load_wp(1, 0)
         load_wp(1, 1)
         load_scales(1)
         load_w(3, E)
 
-        gate_turned = psum.tile([P, PASSES * 2, C], F32, name="gate_turned", tag="bank1")
+        gate_turned = psum.tile([P, PASSES * 2, C], F32, name="gate_turned", tag="bank3")
         for c in range(3):
             nc.tensor.transpose(gate_turned[:, c, :], gate_rows[:, c * P : (c + 1) * P], ident[:])
         nc.scalar.copy(out=gate_cols[:], in_=gate_turned[:, 0:3, 0:2])
@@ -115,10 +116,15 @@ def tile_moe_nxt_lin_none_kernel(tc, xT, w_words, w_scales, wp, gate, offs, out)
 
         s_codes, s_scales = {}, {}
 
-        def gather(a, b, tag=None):
+        def gather(a, b, late=False):
             at = offsets[:, a * C // 16 : b * C // 16]
-            codes = keep.tile([P, (b - a) * C], U32, name=f"s_codes{a}", tag=tag or f"s_codes{a}", align_bytes=64)
-            scales = keep.tile([P, (b - a) * C], U8, name=f"s_scales{a}", align_bytes=64)
+            width = (b - a) * C
+            if late:
+                codes = shared.tile([P, width], U32, name=f"s_codes{a}", offset=0, align_bytes=64)
+                scales = shared.tile([P, width], U8, name=f"s_scales{a}", offset=4 * width, align_bytes=64)
+            else:
+                codes = keep.tile([P, width], U32, name=f"s_codes{a}", align_bytes=64)
+                scales = keep.tile([P, width], U8, name=f"s_scales{a}", align_bytes=64)
             nc.vector.tensor_copy(codes[:], x_codes[:].indirect(at))
             nc.vector.tensor_copy(scales[:], x_scales[:].indirect(at))
             for e in range(a, b):
@@ -128,9 +134,9 @@ def tile_moe_nxt_lin_none_kernel(tc, xT, w_words, w_scales, wp, gate, offs, out)
         rows, turned_of, groups, c_quant, sums, landed = {}, {}, {}, {}, {}, {}
 
         def gated_product(e):
-            rows[e] = keep.tile([P, N], BF16, name=f"c_rows{e}", tag=f"rows{e}", align_bytes=64)
-            i = 0 if e < w_groups[0][1] else 1
+            i = e // w_groups[0][1]
             for g in range(PASSES):
+                rows[e, g] = keep.tile([P, 512], BF16, name=f"c_rows{e}{g}", tag=f"rows{e}{g}", align_bytes=64)
                 y = psum_y.tile([P, 512], F32, name="y")
                 nc.tensor.matmul_mx(
                     out=y[:],
@@ -142,23 +148,27 @@ def tile_moe_nxt_lin_none_kernel(tc, xT, w_words, w_scales, wp, gate, offs, out)
                     stop=True,
                 )
                 nc.scalar.activation(
-                    out=rows[e][:, 512 * g : 512 * (g + 1)].rearrange("s (u p i) -> s u p i", u=2, i=2),
+                    out=rows[e, g][:].rearrange("s (u p i) -> s u p i", u=2, i=2),
                     in_=y[:].rearrange("s (p u i) -> s u p i", u=2, i=2),
                     func=COPY,
                     scale=gate_cols[:, e % 3, e // 3 : e // 3 + 1],
                 )
 
-        def turn(unit, e, bank):
-            turned = psum.tile([P, PASSES * 2, C], F32, name=f"turned{e}", tag=f"bank{bank}")
-            words = rows[e][:].bitcast(F32)
-            for h in range(PASSES * 2):
-                nc.tensor.transpose(turned[:, h, :], words[:, C * h : C * (h + 1)], ident[:])
+        def turn(unit, e, bank, passes=(0, 1)):
+            turned = psum.tile([P, len(passes), 2, C], F32, name=f"turned{e}{passes[0]}", tag=f"bank{bank}")
+            for i, g in enumerate(passes):
+                words = rows[e, g][:].bitcast(F32)
+                for u in range(2):
+                    nc.tensor.transpose(turned[:, i, u, :], words[:, C * u : C * (u + 1)], ident[:])
             width = len(unit) * C
-            if e == unit[0]:
-                groups[unit] = keep.tile([P, PASSES, width, PACK], BF16, name=f"c_group{e}", tag=f"group{e}", align_bytes=64)
+            if unit not in groups:
+                if e == 0:
+                    groups[unit] = shared.tile([P, PASSES, width, PACK], BF16, name="c_group0", offset=0, align_bytes=64)
+                else:
+                    groups[unit] = keep.tile([P, PASSES, width, PACK], BF16, name=f"c_group{e}", align_bytes=64)
             pairs = groups[unit][:].rearrange("p g s j -> p (g s j)").bitcast(F32).rearrange("p (g s u) -> p g s u", g=PASSES, u=2)
             at = (e - unit[0]) * C
-            nc.scalar.copy(out=pairs[:, :, at : at + C, :], in_=turned[:].rearrange("p (g u) s -> p g s u", u=2))
+            nc.scalar.copy(out=pairs[:, passes[0] : passes[-1] + 1, at : at + C, :], in_=turned[:].rearrange("p g u s -> p g s u"))
 
         def quantise_c(unit):
             width = len(unit) * C
@@ -172,9 +182,6 @@ def tile_moe_nxt_lin_none_kernel(tc, xT, w_words, w_scales, wp, gate, offs, out)
             c_quant[unit] = (codes, scales)
 
         wp_group, wp_quant = {}, {}
-
-        def pool_copy(out, in_):
-            nc.gpsimd.tensor_scalar(out, in_, 1.0, 0.0, MULT, mybir.AluOpType.add)
 
         def group_wp(half, g, copy):
             if g == 0:
@@ -231,33 +238,34 @@ def tile_moe_nxt_lin_none_kernel(tc, xT, w_words, w_scales, wp, gate, offs, out)
         group_wp(0, 0, nc.scalar.copy)
         gated_product(0)
         gather(1, 3)
-        turn(u0, 0, 0)
+        turn(u0, 0, 0, (0,))
+        turn(u0, 0, 1, (1,))
         quantise_wp(0, (0,))
         group_wp(0, 1, nc.vector.tensor_copy)
         quantise_wp(0, (1,))
         quantise_c(u0)
+        gather(3, E, late=True)
         gated_product(1)
-        turn(u1, 1, 1)
+        turn(u1, 1, 2)
         quantise_c(u1)
-        gather(3, E, tag="group1")
+        project((u0,), low, 0, tag="rows11")
         gated_product(2)
-        turn(u2, 2, 0)
+        turn(u2, 2, 1)
         quantise_c(u2)
-        group_wp(1, 0, pool_copy)
-        group_wp(1, 1, nc.vector.tensor_copy)
-        for g in range(PASSES):
-            quantise_wp(1, (g,))
-        project((u0,), low, 1)
-        project((u0,), high, 2)
-        project((u1,), low + high, 3, tag="rows2")
+        project((u1,), low, 3)
+        group_wp(1, 0, nc.vector.tensor_copy)
+        group_wp(1, 1, nc.scalar.copy)
+        quantise_wp(1, (0, 1))
+        project((u2,), low, 2, tag="wp_raw11")
         gated_product(3)
         turn(u3, 3, 1)
         quantise_c(u3)
-        project((u2,), low + high, 1)
+        project((u0, u1, u2), high[:1], 0, tag="rows31")
+        project((u0, u1, u2), high[1:], 3)
         for e in u45:
             gated_product(e)
-            turn(u45, e, e - 2)
+            turn(u45, e, 6 - e)
         quantise_c(u45)
-        project((u3,), low + high, 3)
-        project((u45,), low, 0)
-        project((u45,), high, 1)
+        project((u3,), low + high, 0, tag="rows51")
+        project((u45,), low, 2)
+        project((u45,), high, 3)

@@ -89,16 +89,17 @@ def tile_moe_nxt_lin_none_kernel(tc, xT, w_words, w_scales, wp, gate, offs, out)
             nc.sync.dma_start(out=raw[:], in_=wp_view[g, :, :, half * half_width : (half + 1) * half_width])
             wp_raw[half, g] = raw
 
+        load_w(0, 1)
         load_scales(0)
         load_wp(0, 0)
-        load_w(0, 1)
         load_wp(0, 1)
         load_w(1, 2)
         load_w(2, 3)
         load_wp(1, 0)
         load_wp(1, 1)
         load_scales(1)
-        load_w(3, E)
+        load_w(3, 4)
+        load_w(4, E)
 
         gate_turned = psum.tile([P, PASSES * 2, C], F32, name="gate_turned", tag="bank3")
         for c in range(3):
@@ -183,22 +184,17 @@ def tile_moe_nxt_lin_none_kernel(tc, xT, w_words, w_scales, wp, gate, offs, out)
 
         wp_group, wp_quant = {}, {}
 
-        def group_wp(half, g, copy):
-            if g == 0:
-                wp_group[half] = keep.tile([P, PASSES, half_width * PACK], BF16, name=f"wp_group{half}", tag=f"wp_group{half}", align_bytes=64)
-            interleave(copy, wp_group[half][:, g, :], wp_raw[half, g], 0, half_width)
+        def group_wp(half, g, copy, tile=None):
+            if tile is None:
+                tile = keep.tile([P, half_width * PACK], BF16, name=f"wp_group{half}{g}", align_bytes=64)
+            wp_group[half, g] = tile
+            interleave(copy, tile[:], wp_raw[half, g], 0, half_width)
 
-        def quantise_wp(half, passes, tag=None):
-            label = f"wp_codes{half}{passes[0]}"
-            codes = keep.tile([P, len(passes), half_width], U32, name=label, tag=tag or label, align_bytes=64)
-            scales = keep.tile([P, len(passes), half_width], U8, name=f"wp_scales{half}{passes[0]}", align_bytes=64)
-            nc.vector.quantize_mx(
-                out=codes[:].rearrange("p g f -> p (g f)").bitcast(FP8X4),
-                scales=scales[:].rearrange("p g f -> p (g f)"),
-                in_=wp_group[half][:, passes[0] : passes[-1] + 1, :].rearrange("p g f -> p (g f)"),
-            )
-            for i, g in enumerate(passes):
-                wp_quant[half, g] = (codes[:, i, :], scales[:, i, :])
+        def quantise_wp(half, g):
+            codes = keep.tile([P, half_width], U32, name=f"wp_codes{half}{g}", align_bytes=64)
+            scales = keep.tile([P, half_width], U8, name=f"wp_scales{half}{g}", align_bytes=64)
+            nc.vector.quantize_mx(out=codes[:].bitcast(FP8X4), scales=scales[:], in_=wp_group[half, g][:])
+            wp_quant[half, g] = (codes, scales)
 
         windows = [keep.tile([P, T], F32, name=f"window{f}") for f in range(F_TILES)]
 
@@ -235,27 +231,28 @@ def tile_moe_nxt_lin_none_kernel(tc, xT, w_words, w_scales, wp, gate, offs, out)
         u0, u1, u2, u3, u45 = (0,), (1,), (2,), (3,), (4, 5)
 
         gather(0, 1)
-        group_wp(0, 0, nc.scalar.copy)
         gated_product(0)
         gather(1, 3)
+        group_wp(0, 0, nc.vector.tensor_copy)
         turn(u0, 0, 0, (0,))
         turn(u0, 0, 1, (1,))
-        quantise_wp(0, (0,))
+        quantise_wp(0, 0)
         group_wp(0, 1, nc.vector.tensor_copy)
-        quantise_wp(0, (1,))
+        quantise_wp(0, 1)
         quantise_c(u0)
         gather(3, E, late=True)
+        group_wp(1, 0, nc.vector.tensor_copy, shared.tile([P, half_width * PACK], BF16, name="wp_group10", offset=1984, align_bytes=64))
         gated_product(1)
         turn(u1, 1, 2)
         quantise_c(u1)
+        quantise_wp(1, 0)
         project((u0,), low, 0, tag="rows11")
         gated_product(2)
         turn(u2, 2, 1)
         quantise_c(u2)
         project((u1,), low, 3)
-        group_wp(1, 0, nc.vector.tensor_copy)
-        group_wp(1, 1, nc.scalar.copy)
-        quantise_wp(1, (0, 1))
+        group_wp(1, 1, nc.scalar.copy, keep.tile([P, half_width * PACK], BF16, name="wp_group11", tag="rows21", align_bytes=64))
+        quantise_wp(1, 1)
         project((u2,), low, 2, tag="wp_raw11")
         gated_product(3)
         turn(u3, 3, 1)

@@ -55,7 +55,7 @@ def tile_moe_nxt_lin_none_kernel(tc, xT, w_words, w_scales, wp, gate, offs, out)
         make_identity(nc, ident[:])
 
         x_view = xT.rearrange("(p j) t -> p j t", j=PACK)
-        x_cuts = ((0, 256), (256, 512), (512, T))
+        x_cuts = ((0, 512), (512, T))
         x_raw = []
         for a, b in x_cuts:
             raw = keep.tile([P, PACK, b - a], F32, name=f"x_raw{a}")
@@ -92,9 +92,8 @@ def tile_moe_nxt_lin_none_kernel(tc, xT, w_words, w_scales, wp, gate, offs, out)
         load_w(0, 1)
         load_scales(0)
         load_wp(0, 0)
+        load_w(1, 3)
         load_wp(0, 1)
-        load_w(1, 2)
-        load_w(2, 3)
         load_wp(1, 0)
         load_wp(1, 1)
         load_scales(1)
@@ -107,10 +106,9 @@ def tile_moe_nxt_lin_none_kernel(tc, xT, w_words, w_scales, wp, gate, offs, out)
         nc.scalar.copy(out=gate_cols[:], in_=gate_turned[:, 0:3, 0:2])
 
         x_group = keep.tile([P, PACK * T], BF16, name="x_group", align_bytes=64)
-        for (a, b), raw in zip(x_cuts, x_raw):
+        for (a, b), raw, cut in zip(x_cuts, x_raw, (160, 128)):
             width = b - a
             dst = x_group[:, PACK * a : PACK * b]
-            cut = 96
             interleave(nc.scalar.copy, dst, raw, 0, cut)
             interleave(nc.vector.tensor_copy, dst, raw, cut, width)
             nc.vector.quantize_mx(out=x_codes[:, a:b].bitcast(FP8X4), scales=x_scales[:, a:b], in_=dst)
@@ -122,10 +120,9 @@ def tile_moe_nxt_lin_none_kernel(tc, xT, w_words, w_scales, wp, gate, offs, out)
             width = (b - a) * C
             if late:
                 codes = shared.tile([P, width], U32, name=f"s_codes{a}", offset=0, align_bytes=64)
-                scales = shared.tile([P, width], U8, name=f"s_scales{a}", offset=4 * width, align_bytes=64)
             else:
                 codes = keep.tile([P, width], U32, name=f"s_codes{a}", align_bytes=64)
-                scales = keep.tile([P, width], U8, name=f"s_scales{a}", align_bytes=64)
+            scales = keep.tile([P, width], U8, name=f"s_scales{a}", align_bytes=64)
             nc.vector.tensor_copy(codes[:], x_codes[:].indirect(at))
             nc.vector.tensor_copy(scales[:], x_scales[:].indirect(at))
             for e in range(a, b):
@@ -240,7 +237,7 @@ def tile_moe_nxt_lin_none_kernel(tc, xT, w_words, w_scales, wp, gate, offs, out)
         group_wp(0, 1, nc.vector.tensor_copy)
         quantise_wp(0, 1)
         quantise_c(u0)
-        gather(3, E, late=True)
+        gather(3, E)
         group_wp(1, 0, nc.vector.tensor_copy, shared.tile([P, half_width * PACK], BF16, name="wp_group10", offset=1984, align_bytes=64))
         gated_product(1)
         turn(u1, 1, 2)

@@ -225,7 +225,7 @@ def tile_moe_nxt_lin_none_kernel(tc, xT, w_words, w_scales, wp, gate, offs, out)
                     nc.sync.dma_start(out=out[f * P : (f + 1) * P, :], in_=windows[f][:])
 
         low, high = (0, 1), (2, 3)
-        u0, u1, u2, u3, u45 = (0,), (1,), (2,), (3,), (4, 5)
+        u0, u1, u2, u3, u4, u5 = ((e,) for e in range(E))
 
         gather(0, 1)
         gated_product(0)
@@ -256,10 +256,14 @@ def tile_moe_nxt_lin_none_kernel(tc, xT, w_words, w_scales, wp, gate, offs, out)
         quantise_c(u3)
         project((u0, u1, u2), high[:1], 0, tag="rows31")
         project((u0, u1, u2), high[1:], 3)
-        for e in u45:
-            gated_product(e)
-            turn(u45, e, 6 - e)
-        quantise_c(u45)
-        project((u3,), low + high, 0, tag="rows51")
-        project((u45,), low, 2)
-        project((u45,), high, 3)
+        gated_product(4)
+        turn(u4, 4, 2)
+        quantise_c(u4)
+        project((u3,), low + high, 0, tag="rows41")
+        gated_product(5)
+        turn(u5, 5, 1)
+        quantise_c(u5)
+        project((u4,), low, 3, tag="rows51")
+        project((u5,), low, 2)
+        project((u4, u5), high[:1], 0)
+        project((u4, u5), high[1:], 1)

@@ -6,8 +6,14 @@ from concourse.masks import make_identity
 K, T, E, C, N, M = 512, 768, 6, 128, 1024, 512
 P = 128
 PACK = 4
-PASSES = N // 512
+PASS = P * PACK
+PASSES = N // PASS
 F_TILES = M // P
+HALF = M // 2
+GATE_ROWS = 2
+PER_ROW = E // GATE_ROWS
+SCALE_GROUP = 3
+X_CHUNKS = ((0, 512, 160), (512, T, 128))
 
 FLOPS = 2 * K * N * E * C + 2 * N * M * T
 BYTES = 4 * K * T + E * K * N // 2 + E * (K // 32) * N + 4 * N * M + 4 * E * C + 2 * E * C + 4 * M * T
@@ -21,7 +27,6 @@ U8 = mybir.dt.uint8
 FP8X4 = mybir.dt.float8_e4m3fn_x4
 FP4X4 = mybir.dt.float4_e2m1fn_x4
 COPY = mybir.ActivationFunctionType.Copy
-MULT = mybir.AluOpType.mult
 
 
 def interleave(copy, dst, src, a, b):
@@ -35,35 +40,36 @@ def tile_moe_nxt_lin_none_kernel(tc, xT, w_words, w_scales, wp, gate, offs, out)
     nc = tc.nc
     with ExitStack() as ctx:
         keep = ctx.enter_context(tc.tile_pool(name="keep", bufs=1))
-        shared = ctx.enter_context(tc.tile_pool(name="shared", bufs=1))
         psum_y = ctx.enter_context(tc.psum_pool(name="psum_y", bufs=4))
         psum = ctx.enter_context(tc.psum_pool(name="psum", bufs=1))
 
         offsets = keep.tile([P, E * C // 16], U16, name="offsets")
-        gate_cols = keep.tile([P, 3, 2], F32, name="gate_cols")
-        gate_rows = keep.tile([P, 3 * P], F32, name="gate_rows")
+        gate_cols = keep.tile([P, PER_ROW, GATE_ROWS], F32, name="gate_cols")
+        gate_rows = keep.tile([P, PER_ROW * C], F32, name="gate_rows")
         ident = keep.tile([P, P], F32, name="ident")
         x_codes = keep.tile([P, T], U32, name="x_codes", align_bytes=64)
         x_scales = keep.tile([P, T], U8, name="x_scales", align_bytes=64)
-        w_groups = ((0, 3), (3, E))
-        w_planes = [keep.tile([P, b - a, N], U8, name=f"w_planes{a}", align_bytes=64) for a, b in w_groups]
+        w_scale_tiles = [
+            keep.tile([P, SCALE_GROUP, N], U8, name=f"w_scales{i}", align_bytes=64) for i in range(E // SCALE_GROUP)
+        ]
 
         nc.gpsimd.memset(gate_rows[:], 0.0)
-        for planes in w_planes:
-            nc.vector.memset(planes[:].rearrange("p e n -> p (e n)").bitcast(I32), 0)
+        for tile in w_scale_tiles:
+            nc.vector.memset(tile[:].rearrange("p e n -> p (e n)").bitcast(I32), 0)
         nc.gpsimd.memset(x_scales[:], 0)
         make_identity(nc, ident[:])
 
         x_view = xT.rearrange("(p j) t -> p j t", j=PACK)
-        x_cuts = ((0, 512), (512, T))
         x_raw = []
-        for a, b in x_cuts:
+        for a, b, share in X_CHUNKS:
             raw = keep.tile([P, PACK, b - a], F32, name=f"x_raw{a}")
             nc.sync.dma_start(out=raw[:], in_=x_view[:, :, a:b])
             x_raw.append(raw)
             if a == 0:
                 nc.sync.dma_start(offsets[:], offs)
-                nc.sync.dma_start(out=gate_rows[0:2, :], in_=gate[0:1, :].rearrange("o (r s) -> (o r) s", r=2))
+                nc.sync.dma_start(
+                    out=gate_rows[0:GATE_ROWS, :], in_=gate[0:1, :].rearrange("o (r s) -> (o r) s", r=GATE_ROWS)
+                )
 
         w_codes = {}
 
@@ -76,18 +82,19 @@ def tile_moe_nxt_lin_none_kernel(tc, xT, w_words, w_scales, wp, gate, offs, out)
         scale_rows = w_scales.bitcast(I32).rearrange("e a (q r) n -> r q (e a) n", r=4)
 
         def load_scales(i):
-            a, b = w_groups[i]
             for r in range(4):
-                nc.sync.dma_start(out=w_planes[i][r:P:32, :, :].bitcast(I32), in_=scale_rows[r, :, a:b, :])
+                nc.sync.dma_start(
+                    out=w_scale_tiles[i][r:P:32, :, :].bitcast(I32),
+                    in_=scale_rows[r, :, i * SCALE_GROUP : (i + 1) * SCALE_GROUP, :],
+                )
 
         wp_view = wp.rearrange("(g p j) f -> g p j f", p=P, j=PACK)
-        half_width = M // 2
         wp_raw = {}
 
         def load_wp(half, g):
-            raw = keep.tile([P, PACK, half_width], F32, name=f"wp_raw{half}{g}", tag=f"wp_raw{half}{g}", align_bytes=64)
-            nc.sync.dma_start(out=raw[:], in_=wp_view[g, :, :, half * half_width : (half + 1) * half_width])
-            wp_raw[half, g] = raw
+            label = f"wp_raw{half}{g}"
+            wp_raw[half, g] = keep.tile([P, PACK, HALF], F32, name=label, tag=label, align_bytes=64)
+            nc.sync.dma_start(out=wp_raw[half, g][:], in_=wp_view[g, :, :, half * HALF : (half + 1) * HALF])
 
         load_w(0, 1)
         load_scales(0)
@@ -101,47 +108,41 @@ def tile_moe_nxt_lin_none_kernel(tc, xT, w_words, w_scales, wp, gate, offs, out)
         load_w(4, E)
 
         gate_turned = psum.tile([P, PASSES * 2, C], F32, name="gate_turned", tag="bank3")
-        for c in range(3):
-            nc.tensor.transpose(gate_turned[:, c, :], gate_rows[:, c * P : (c + 1) * P], ident[:])
-        nc.scalar.copy(out=gate_cols[:], in_=gate_turned[:, 0:3, 0:2])
+        for c in range(PER_ROW):
+            nc.tensor.transpose(gate_turned[:, c, :], gate_rows[:, c * C : (c + 1) * C], ident[:])
+        nc.scalar.copy(out=gate_cols[:], in_=gate_turned[:, 0:PER_ROW, 0:GATE_ROWS])
 
         x_group = keep.tile([P, PACK * T], BF16, name="x_group", align_bytes=64)
-        for (a, b), raw, cut in zip(x_cuts, x_raw, (160, 128)):
-            width = b - a
+        for (a, b, share), raw in zip(X_CHUNKS, x_raw):
             dst = x_group[:, PACK * a : PACK * b]
-            interleave(nc.scalar.copy, dst, raw, 0, cut)
-            interleave(nc.vector.tensor_copy, dst, raw, cut, width)
+            interleave(nc.scalar.copy, dst, raw, 0, share)
+            interleave(nc.vector.tensor_copy, dst, raw, share, b - a)
             nc.vector.quantize_mx(out=x_codes[:, a:b].bitcast(FP8X4), scales=x_scales[:, a:b], in_=dst)
 
-        s_codes, s_scales = {}, {}
+        s_codes, s_scales, rows, c_groups, c_quant, wp_groups, wp_quant = {}, {}, {}, {}, {}, {}, {}
 
-        def gather(a, b, late=False):
-            at = offsets[:, a * C // 16 : b * C // 16]
-            width = (b - a) * C
-            if late:
-                codes = shared.tile([P, width], U32, name=f"s_codes{a}", offset=0, align_bytes=64)
-            else:
-                codes = keep.tile([P, width], U32, name=f"s_codes{a}", align_bytes=64)
-            scales = keep.tile([P, width], U8, name=f"s_scales{a}", align_bytes=64)
-            nc.vector.tensor_copy(codes[:], x_codes[:].indirect(at))
-            nc.vector.tensor_copy(scales[:], x_scales[:].indirect(at))
+        def slots(a, b):
+            return offsets[:, a * C // 16 : b * C // 16]
+
+        def gather(a, b):
+            codes = keep.tile([P, (b - a) * C], U32, name=f"s_codes{a}", align_bytes=64)
+            scales = keep.tile([P, (b - a) * C], U8, name=f"s_scales{a}", align_bytes=64)
+            nc.vector.tensor_copy(codes[:], x_codes[:].indirect(slots(a, b)))
+            nc.vector.tensor_copy(scales[:], x_scales[:].indirect(slots(a, b)))
             for e in range(a, b):
                 s_codes[e] = codes[:, (e - a) * C : (e - a + 1) * C]
                 s_scales[e] = scales[:, (e - a) * C : (e - a + 1) * C]
 
-        rows, turned_of, groups, c_quant, sums, landed = {}, {}, {}, {}, {}, {}
-
         def gated_product(e):
-            i = e // w_groups[0][1]
             for g in range(PASSES):
-                rows[e, g] = keep.tile([P, 512], BF16, name=f"c_rows{e}{g}", tag=f"rows{e}{g}", align_bytes=64)
-                y = psum_y.tile([P, 512], F32, name="y")
+                rows[e, g] = keep.tile([P, PASS], BF16, name=f"c_rows{e}{g}", tag=f"rows{e}{g}", align_bytes=64)
+                y = psum_y.tile([P, PASS], F32, name="y")
                 nc.tensor.matmul_mx(
                     out=y[:],
                     lhsT=s_codes[e].bitcast(FP8X4),
                     lhsT_scale=s_scales[e],
-                    rhs=w_codes[e][:, 1024 * g : 1024 * (g + 1)].bitcast(FP4X4),
-                    rhs_scale=w_planes[i][:, e - w_groups[i][0], 512 * g : 512 * (g + 1)],
+                    rhs=w_codes[e][:, 2 * PASS * g : 2 * PASS * (g + 1)].bitcast(FP4X4),
+                    rhs_scale=w_scale_tiles[e // SCALE_GROUP][:, e % SCALE_GROUP, PASS * g : PASS * (g + 1)],
                     start=True,
                     stop=True,
                 )
@@ -149,121 +150,110 @@ def tile_moe_nxt_lin_none_kernel(tc, xT, w_words, w_scales, wp, gate, offs, out)
                     out=rows[e, g][:].rearrange("s (u p i) -> s u p i", u=2, i=2),
                     in_=y[:].rearrange("s (p u i) -> s u p i", u=2, i=2),
                     func=COPY,
-                    scale=gate_cols[:, e % 3, e // 3 : e // 3 + 1],
+                    scale=gate_cols[:, e % PER_ROW, e // PER_ROW : e // PER_ROW + 1],
                 )
 
-        def turn(unit, e, bank, passes=(0, 1)):
+        def turn(e, bank, passes=(0, 1)):
             turned = psum.tile([P, len(passes), 2, C], F32, name=f"turned{e}{passes[0]}", tag=f"bank{bank}")
             for i, g in enumerate(passes):
                 words = rows[e, g][:].bitcast(F32)
                 for u in range(2):
-                    nc.tensor.transpose(turned[:, i, u, :], words[:, C * u : C * (u + 1)], ident[:])
-            width = len(unit) * C
-            if unit not in groups:
-                if e == 0:
-                    groups[unit] = shared.tile([P, PASSES, width, PACK], BF16, name="c_group0", offset=0, align_bytes=64)
-                else:
-                    groups[unit] = keep.tile([P, PASSES, width, PACK], BF16, name=f"c_group{e}", align_bytes=64)
-            pairs = groups[unit][:].rearrange("p g s j -> p (g s j)").bitcast(F32).rearrange("p (g s u) -> p g s u", g=PASSES, u=2)
-            at = (e - unit[0]) * C
-            nc.scalar.copy(out=pairs[:, passes[0] : passes[-1] + 1, at : at + C, :], in_=turned[:].rearrange("p g u s -> p g s u"))
+                    nc.tensor.transpose(turned[:, i, u, :], words[:, P * u : P * (u + 1)], ident[:])
+            if e not in c_groups:
+                c_groups[e] = keep.tile([P, PASSES, C, PACK], BF16, name=f"c_group{e}", tag=f"c_group{e}", align_bytes=64)
+            pairs = c_groups[e][:].rearrange("p g s j -> p (g s j)").bitcast(F32)
+            pairs = pairs.rearrange("p (g s u) -> p g s u", g=PASSES, u=2)
+            nc.scalar.copy(out=pairs[:, passes[0] : passes[-1] + 1, :, :], in_=turned[:].rearrange("p g u s -> p g s u"))
 
-        def quantise_c(unit):
-            width = len(unit) * C
-            codes = keep.tile([P, PASSES, width], U32, name=f"c_codes{unit[0]}", align_bytes=64)
-            scales = keep.tile([P, PASSES, width], U8, name=f"c_scales{unit[0]}", align_bytes=64)
+        def quantise_c(e):
+            codes = keep.tile([P, PASSES, C], U32, name=f"c_codes{e}", align_bytes=64)
+            scales = keep.tile([P, PASSES, C], U8, name=f"c_scales{e}", align_bytes=64)
             nc.vector.quantize_mx(
                 out=codes[:].rearrange("p g s -> p (g s)").bitcast(FP8X4),
                 scales=scales[:].rearrange("p g s -> p (g s)"),
-                in_=groups[unit][:].rearrange("p g s j -> p (g s j)"),
+                in_=c_groups[e][:].rearrange("p g s j -> p (g s j)"),
             )
-            c_quant[unit] = (codes, scales)
+            c_quant[e] = (codes, scales)
 
-        wp_group, wp_quant = {}, {}
-
-        def group_wp(half, g, copy, tile=None):
-            if tile is None:
-                tile = keep.tile([P, half_width * PACK], BF16, name=f"wp_group{half}{g}", align_bytes=64)
-            wp_group[half, g] = tile
-            interleave(copy, tile[:], wp_raw[half, g], 0, half_width)
+        def group_wp(half, g, copy, buffer=None):
+            label = f"wp_group{half}{g}"
+            wp_groups[half, g] = keep.tile([P, HALF * PACK], BF16, name=label, tag=buffer or label, align_bytes=64)
+            interleave(copy, wp_groups[half, g][:], wp_raw[half, g], 0, HALF)
 
         def quantise_wp(half, g):
-            codes = keep.tile([P, half_width], U32, name=f"wp_codes{half}{g}", align_bytes=64)
-            scales = keep.tile([P, half_width], U8, name=f"wp_scales{half}{g}", align_bytes=64)
-            nc.vector.quantize_mx(out=codes[:].bitcast(FP8X4), scales=scales[:], in_=wp_group[half, g][:])
+            codes = keep.tile([P, HALF], U32, name=f"wp_codes{half}{g}", align_bytes=64)
+            scales = keep.tile([P, HALF], U8, name=f"wp_scales{half}{g}", align_bytes=64)
+            nc.vector.quantize_mx(out=codes[:].bitcast(FP8X4), scales=scales[:], in_=wp_groups[half, g][:])
             wp_quant[half, g] = (codes, scales)
 
         windows = [keep.tile([P, T], F32, name=f"window{f}") for f in range(F_TILES)]
 
-        def project(units, f_tiles, bank, tag=None):
-            width = sum(len(unit) for unit in units) * C
-            o = psum.tile([P, 512], F32, name=f"o{units[0][0]}{f_tiles[0]}", tag=f"bank{bank}")
+        def project(a, b, f_tiles, bank, buffer=None):
+            width = (b - a) * C
+            sums = psum.tile([P, 512], F32, name=f"sums{a}{f_tiles[0]}", tag=f"bank{bank}")
             for i, f in enumerate(f_tiles):
                 half, at = f // 2, (f % 2) * P
-                col = i * width
-                for unit in units:
-                    codes, scales = c_quant[unit]
+                for e in range(a, b):
+                    col = i * width + (e - a) * C
                     for g in range(PASSES):
                         nc.tensor.matmul_mx(
-                            out=o[:, col : col + len(unit) * C],
+                            out=sums[:, col : col + C],
                             lhsT=wp_quant[half, g][0][:, at : at + P].bitcast(FP8X4),
                             lhsT_scale=wp_quant[half, g][1][:, at : at + P],
-                            rhs=codes[:, g, :].bitcast(FP8X4),
-                            rhs_scale=scales[:, g, :],
+                            rhs=c_quant[e][0][:, g, :].bitcast(FP8X4),
+                            rhs_scale=c_quant[e][1][:, g, :],
                             start=(g == 0),
                             stop=(g == PASSES - 1),
                         )
-                    col = col + len(unit) * C
-            label = f"landed{units[0][0]}{f_tiles[0]}"
-            landed = keep.tile([P, len(f_tiles), width], F32, name=label, tag=tag or label, align_bytes=64)
-            nc.scalar.copy(out=landed[:].rearrange("p f s -> p (f s)"), in_=o[:, : len(f_tiles) * width])
-            sums[units[0][0], f_tiles[0]] = landed
-            a, b = units[0][0], units[-1][-1] + 1
+            label = f"landed{a}{f_tiles[0]}"
+            landed = keep.tile([P, len(f_tiles), width], F32, name=label, tag=buffer or label, align_bytes=64)
+            nc.scalar.copy(out=landed[:].rearrange("p f s -> p (f s)"), in_=sums[:, : len(f_tiles) * width])
             for i, f in enumerate(f_tiles):
-                nc.vector.tensor_copy(windows[f][:].indirect(offsets[:, a * C // 16 : b * C // 16]), landed[:, i, :])
+                nc.vector.tensor_copy(windows[f][:].indirect(slots(a, b)), landed[:, i, :])
                 if b == E:
                     nc.sync.dma_start(out=out[f * P : (f + 1) * P, :], in_=windows[f][:])
 
-        low, high = (0, 1), (2, 3)
-        u0, u1, u2, u3, u4, u5 = ((e,) for e in range(E))
+        lower = (0, 1)
 
         gather(0, 1)
         gated_product(0)
         gather(1, 3)
         group_wp(0, 0, nc.vector.tensor_copy)
-        turn(u0, 0, 0, (0,))
-        turn(u0, 0, 1, (1,))
+        turn(0, 0, (0,))
+        turn(0, 1, (1,))
         quantise_wp(0, 0)
         group_wp(0, 1, nc.vector.tensor_copy)
         quantise_wp(0, 1)
-        quantise_c(u0)
+        quantise_c(0)
         gather(3, E)
-        group_wp(1, 0, nc.vector.tensor_copy, shared.tile([P, half_width * PACK], BF16, name="wp_group10", offset=1984, align_bytes=64))
+        group_wp(1, 0, nc.vector.tensor_copy, buffer="c_group0")
+
         gated_product(1)
-        turn(u1, 1, 2)
-        quantise_c(u1)
+        turn(1, 2)
+        quantise_c(1)
         quantise_wp(1, 0)
-        project((u0,), low, 0, tag="rows11")
+        project(0, 1, lower, 0, buffer="rows11")
         gated_product(2)
-        turn(u2, 2, 1)
-        quantise_c(u2)
-        project((u1,), low, 3)
-        group_wp(1, 1, nc.scalar.copy, keep.tile([P, half_width * PACK], BF16, name="wp_group11", tag="rows21", align_bytes=64))
+        turn(2, 1)
+        quantise_c(2)
+        project(1, 2, lower, 3)
+        group_wp(1, 1, nc.scalar.copy, buffer="rows21")
         quantise_wp(1, 1)
-        project((u2,), low, 2, tag="wp_raw11")
+        project(2, 3, lower, 2, buffer="wp_raw11")
         gated_product(3)
-        turn(u3, 3, 1)
-        quantise_c(u3)
-        project((u0, u1, u2), high[:1], 0, tag="rows31")
-        project((u0, u1, u2), high[1:], 3)
+        turn(3, 1)
+        quantise_c(3)
+        project(0, 3, (2,), 0, buffer="rows31")
+        project(0, 3, (3,), 3)
+
         gated_product(4)
-        turn(u4, 4, 2)
-        quantise_c(u4)
-        project((u3,), low + high, 0, tag="rows41")
+        turn(4, 2)
+        quantise_c(4)
+        project(3, 4, (0, 1, 2, 3), 0, buffer="rows41")
         gated_product(5)
-        turn(u5, 5, 1)
-        quantise_c(u5)
-        project((u4,), low, 3, tag="rows51")
-        project((u5,), low, 2)
-        project((u4, u5), high[:1], 0)
-        project((u4, u5), high[1:], 1)
+        turn(5, 1)
+        quantise_c(5)
+        project(4, 5, lower, 3, buffer="rows51")
+        project(5, 6, lower, 2)
+        project(4, 6, (2,), 0)
+        project(4, 6, (3,), 1)

@@ -40,7 +40,6 @@ def tile_moe_nxt_lin_none_kernel(tc, xT, w_words, w_scales, wp, gate, offs, out)
     nc = tc.nc
     with ExitStack() as ctx:
         keep = ctx.enter_context(tc.tile_pool(name="keep", bufs=1))
-        psum_y = ctx.enter_context(tc.psum_pool(name="psum_y", bufs=4))
         psum = ctx.enter_context(tc.psum_pool(name="psum", bufs=1))
 
         offsets = keep.tile([P, E * C // 16], U16, name="offsets")
@@ -96,11 +95,11 @@ def tile_moe_nxt_lin_none_kernel(tc, xT, w_words, w_scales, wp, gate, offs, out)
             wp_raw[half, g] = keep.tile([P, PACK, HALF], F32, name=label, tag=label, align_bytes=64)
             nc.sync.dma_start(out=wp_raw[half, g][:], in_=wp_view[g, :, :, half * HALF : (half + 1) * HALF])
 
-        load_w(0, 1)
+        load_w(0, 2)
         load_scales(0)
         load_wp(0, 0)
-        load_w(1, 3)
         load_wp(0, 1)
+        load_w(2, 3)
         load_wp(1, 0)
         load_wp(1, 1)
         load_scales(1)
@@ -124,9 +123,9 @@ def tile_moe_nxt_lin_none_kernel(tc, xT, w_words, w_scales, wp, gate, offs, out)
         def slots(a, b):
             return offsets[:, a * C // 16 : b * C // 16]
 
-        def gather(a, b):
+        def gather(a, b, buffer=None):
             codes = keep.tile([P, (b - a) * C], U32, name=f"s_codes{a}", align_bytes=64)
-            scales = keep.tile([P, (b - a) * C], U8, name=f"s_scales{a}", align_bytes=64)
+            scales = keep.tile([P, (b - a) * C], U8, name=f"s_scales{a}", tag=buffer or f"s_scales{a}", align_bytes=64)
             nc.vector.tensor_copy(codes[:], x_codes[:].indirect(slots(a, b)))
             nc.vector.tensor_copy(scales[:], x_scales[:].indirect(slots(a, b)))
             for e in range(a, b):
@@ -136,7 +135,7 @@ def tile_moe_nxt_lin_none_kernel(tc, xT, w_words, w_scales, wp, gate, offs, out)
         def gated_product(e):
             for g in range(PASSES):
                 rows[e, g] = keep.tile([P, PASS], BF16, name=f"c_rows{e}{g}", tag=f"rows{e}{g}", align_bytes=64)
-                y = psum_y.tile([P, PASS], F32, name="y")
+                y = psum.tile([P, PASS], F32, name=f"y{e}{g}", tag=f"bank{4 + 2 * (e % 2) + g}")
                 nc.tensor.matmul_mx(
                     out=y[:],
                     lhsT=s_codes[e].bitcast(FP8X4),
@@ -153,38 +152,52 @@ def tile_moe_nxt_lin_none_kernel(tc, xT, w_words, w_scales, wp, gate, offs, out)
                     scale=gate_cols[:, e % PER_ROW, e // PER_ROW : e // PER_ROW + 1],
                 )
 
-        def turn(e, bank, passes=(0, 1)):
-            turned = psum.tile([P, len(passes), 2, C], F32, name=f"turned{e}{passes[0]}", tag=f"bank{bank}")
-            for i, g in enumerate(passes):
+        def turn(e, bank, unit=None):
+            unit = unit or (e, e + 1)
+            turned = psum.tile([P, PASSES, 2, C], F32, name=f"turned{e}", tag=f"bank{bank}")
+            for g in range(PASSES):
                 words = rows[e, g][:].bitcast(F32)
                 for u in range(2):
-                    nc.tensor.transpose(turned[:, i, u, :], words[:, P * u : P * (u + 1)], ident[:])
-            if e not in c_groups:
-                c_groups[e] = keep.tile([P, PASSES, C, PACK], BF16, name=f"c_group{e}", tag=f"c_group{e}", align_bytes=64)
-            pairs = c_groups[e][:].rearrange("p g s j -> p (g s j)").bitcast(F32)
-            pairs = pairs.rearrange("p (g s u) -> p g s u", g=PASSES, u=2)
-            nc.scalar.copy(out=pairs[:, passes[0] : passes[-1] + 1, :, :], in_=turned[:].rearrange("p g u s -> p g s u"))
+                    nc.tensor.transpose(turned[:, g, u, :], words[:, P * u : P * (u + 1)], ident[:])
+            if unit not in c_groups:
+                label = f"c_group{unit[0]}"
+                c_groups[unit] = keep.tile([P, unit[1] - unit[0], N], BF16, name=label, tag=label, align_bytes=64)
+            pairs = c_groups[unit][:, e - unit[0], :].bitcast(F32).rearrange("p (g s u) -> p g s u", g=PASSES, u=2)
+            nc.scalar.copy(out=pairs, in_=turned[:].rearrange("p g u s -> p g s u"))
 
-        def quantise_c(e):
-            codes = keep.tile([P, PASSES, C], U32, name=f"c_codes{e}", align_bytes=64)
-            scales = keep.tile([P, PASSES, C], U8, name=f"c_scales{e}", align_bytes=64)
+        def quantise_c(a, b):
+            codes = keep.tile([P, b - a, PASSES, C], U32, name=f"c_codes{a}", align_bytes=64)
+            scales = keep.tile([P, b - a, PASSES, C], U8, name=f"c_scales{a}", align_bytes=64)
             nc.vector.quantize_mx(
-                out=codes[:].rearrange("p g s -> p (g s)").bitcast(FP8X4),
-                scales=scales[:].rearrange("p g s -> p (g s)"),
-                in_=c_groups[e][:].rearrange("p g s j -> p (g s j)"),
+                out=codes[:].rearrange("p e g s -> p (e g s)").bitcast(FP8X4),
+                scales=scales[:].rearrange("p e g s -> p (e g s)"),
+                in_=c_groups[a, b][:].rearrange("p e n -> p (e n)"),
             )
-            c_quant[e] = (codes, scales)
+            for e in range(a, b):
+                c_quant[e] = (codes[:, e - a], scales[:, e - a])
 
-        def group_wp(half, g, copy, buffer=None):
-            label = f"wp_group{half}{g}"
-            wp_groups[half, g] = keep.tile([P, HALF * PACK], BF16, name=label, tag=buffer or label, align_bytes=64)
-            interleave(copy, wp_groups[half, g][:], wp_raw[half, g], 0, HALF)
+        def group_wp(a, b, g, copy, buffer=None):
+            if (a, b) not in wp_groups:
+                label = f"wp_group{a}"
+                wp_groups[a, b] = keep.tile(
+                    [P, b - a, PASSES, P * PACK], BF16, name=label, tag=buffer or label, align_bytes=64
+                )
+            at = (a % 2) * P
+            copy(
+                out=wp_groups[a, b][:, :, g, :].rearrange("p f (c i j) -> p f c j i", i=4, j=PACK),
+                in_=wp_raw[a // 2, g][:, :, at : at + (b - a) * P].rearrange("p j (f c i) -> p f c j i", f=b - a, i=4),
+            )
 
-        def quantise_wp(half, g):
-            codes = keep.tile([P, HALF], U32, name=f"wp_codes{half}{g}", align_bytes=64)
-            scales = keep.tile([P, HALF], U8, name=f"wp_scales{half}{g}", align_bytes=64)
-            nc.vector.quantize_mx(out=codes[:].bitcast(FP8X4), scales=scales[:], in_=wp_groups[half, g][:])
-            wp_quant[half, g] = (codes, scales)
+        def quantise_wp(a, b):
+            codes = keep.tile([P, b - a, PASSES, P], U32, name=f"wp_codes{a}", align_bytes=64)
+            scales = keep.tile([P, b - a, PASSES, P], U8, name=f"wp_scales{a}", align_bytes=64)
+            nc.vector.quantize_mx(
+                out=codes[:].rearrange("p f g c -> p (f g c)").bitcast(FP8X4),
+                scales=scales[:].rearrange("p f g c -> p (f g c)"),
+                in_=wp_groups[a, b][:].rearrange("p f g c -> p (f g c)"),
+            )
+            for f in range(a, b):
+                wp_quant[f] = (codes[:, f - a], scales[:, f - a])
 
         windows = [keep.tile([P, T], F32, name=f"window{f}") for f in range(F_TILES)]
 
@@ -192,14 +205,13 @@ def tile_moe_nxt_lin_none_kernel(tc, xT, w_words, w_scales, wp, gate, offs, out)
             width = (b - a) * C
             sums = psum.tile([P, 512], F32, name=f"sums{a}{f_tiles[0]}", tag=f"bank{bank}")
             for i, f in enumerate(f_tiles):
-                half, at = f // 2, (f % 2) * P
                 for e in range(a, b):
                     col = i * width + (e - a) * C
                     for g in range(PASSES):
                         nc.tensor.matmul_mx(
                             out=sums[:, col : col + C],
-                            lhsT=wp_quant[half, g][0][:, at : at + P].bitcast(FP8X4),
-                            lhsT_scale=wp_quant[half, g][1][:, at : at + P],
+                            lhsT=wp_quant[f][0][:, g, :].bitcast(FP8X4),
+                            lhsT_scale=wp_quant[f][1][:, g, :],
                             rhs=c_quant[e][0][:, g, :].bitcast(FP8X4),
                             rhs_scale=c_quant[e][1][:, g, :],
                             start=(g == 0),
@@ -218,42 +230,40 @@ def tile_moe_nxt_lin_none_kernel(tc, xT, w_words, w_scales, wp, gate, offs, out)
         gather(0, 1)
         gated_product(0)
         gather(1, 3)
-        group_wp(0, 0, nc.vector.tensor_copy)
-        turn(0, 0, (0,))
-        turn(0, 1, (1,))
-        quantise_wp(0, 0)
-        group_wp(0, 1, nc.vector.tensor_copy)
-        quantise_wp(0, 1)
-        quantise_c(0)
         gather(3, E)
-        group_wp(1, 0, nc.vector.tensor_copy, buffer="c_group0")
-
+        turn(0, 0)
         gated_product(1)
-        turn(1, 2)
-        quantise_c(1)
-        quantise_wp(1, 0)
-        project(0, 1, lower, 0, buffer="rows11")
+        turn(1, 1)
+        for g in range(PASSES):
+            for f in lower:
+                group_wp(f, f + 1, g, nc.vector.tensor_copy)
+        quantise_wp(0, 1)
+        quantise_c(0, 1)
+        quantise_wp(1, 2)
+        quantise_c(1, 2)
+        group_wp(2, 4, 0, nc.vector.tensor_copy, buffer="c_group1")
+        project(0, 1, (0,), 2)
+        project(0, 1, (1,), 3)
         gated_product(2)
-        turn(2, 1)
-        quantise_c(2)
-        project(1, 2, lower, 3)
-        group_wp(1, 1, nc.scalar.copy, buffer="rows21")
-        quantise_wp(1, 1)
-        project(2, 3, lower, 2, buffer="wp_raw11")
+        turn(2, 0)
+        quantise_c(2, 3)
+        project(1, 2, lower, 2, buffer="rows21")
+        group_wp(2, 4, 1, nc.scalar.copy)
+        quantise_wp(2, 4)
+        project(2, 3, lower, 1, buffer="wp_raw11")
         gated_product(3)
-        turn(3, 1)
-        quantise_c(3)
-        project(0, 3, (2,), 0, buffer="rows31")
-        project(0, 3, (3,), 3)
+        turn(3, 3)
+        quantise_c(3, 4)
+        project(0, 3, (2,), 7, buffer="rows31")
+        project(0, 3, (3,), 0)
 
         gated_product(4)
-        turn(4, 2)
-        quantise_c(4)
-        project(3, 4, (0, 1, 2, 3), 0, buffer="rows41")
+        turn(4, 2, (4, 6))
         gated_product(5)
-        turn(5, 1)
-        quantise_c(5)
-        project(4, 5, lower, 3, buffer="rows51")
-        project(5, 6, lower, 2)
-        project(4, 6, (2,), 0)
-        project(4, 6, (3,), 1)
+        turn(5, 0, (4, 6))
+        quantise_c(4, 6)
+        project(3, 4, lower, 1, buffer="rows51")
+        project(4, 6, (0,), 3)
+        project(4, 6, (1,), 2)
+        project(3, 6, (2,), 0)
+        project(3, 6, (3,), 1)

@@ -9,11 +9,10 @@ PACK = 4
 PASS = P * PACK
 PASSES = N // PASS
 F_TILES = M // P
-HALF = M // 2
 GATE_ROWS = 2
 PER_ROW = E // GATE_ROWS
-SCALE_GROUP = 3
-X_CHUNKS = ((0, 512, 160), (512, T, 128))
+SCALE_GROUP = 2
+X_CHUNKS = ((0, 352, 512), (512, 624, T))
 
 FLOPS = 2 * K * N * E * C + 2 * N * M * T
 BYTES = 4 * K * T + E * K * N // 2 + E * (K // 32) * N + 4 * N * M + 4 * E * C + 2 * E * C + 4 * M * T
@@ -59,16 +58,10 @@ def tile_moe_nxt_lin_none_kernel(tc, xT, w_words, w_scales, wp, gate, offs, out)
         make_identity(nc, ident[:])
 
         x_view = xT.rearrange("(p j) t -> p j t", j=PACK)
-        x_raw = []
-        for a, b, share in X_CHUNKS:
-            raw = keep.tile([P, PACK, b - a], F32, name=f"x_raw{a}")
-            nc.sync.dma_start(out=raw[:], in_=x_view[:, :, a:b])
-            x_raw.append(raw)
-            if a == 0:
-                nc.sync.dma_start(offsets[:], offs)
-                nc.sync.dma_start(
-                    out=gate_rows[0:GATE_ROWS, :], in_=gate[0:1, :].rearrange("o (r s) -> (o r) s", r=GATE_ROWS)
-                )
+        x_raw = keep.tile([P, PACK, T], F32, name="x_raw")
+        nc.sync.dma_start(offsets[:], offs)
+        nc.sync.dma_start(out=x_raw[:], in_=x_view)
+        nc.sync.dma_start(out=gate_rows[0:GATE_ROWS, :], in_=gate[0:1, :].rearrange("o (r s) -> (o r) s", r=GATE_ROWS))
 
         w_codes = {}
 
@@ -88,44 +81,41 @@ def tile_moe_nxt_lin_none_kernel(tc, xT, w_words, w_scales, wp, gate, offs, out)
                 )
 
         wp_view = wp.rearrange("(g p j) f -> g p j f", p=P, j=PACK)
-        wp_raw = {}
+        wp_raw = [keep.tile([P, PACK, M], F32, name=f"wp_raw{g}", align_bytes=64) for g in range(PASSES)]
 
-        def load_wp(half, g):
-            label = f"wp_raw{half}{g}"
-            wp_raw[half, g] = keep.tile([P, PACK, HALF], F32, name=label, tag=label, align_bytes=64)
-            nc.sync.dma_start(out=wp_raw[half, g][:], in_=wp_view[g, :, :, half * HALF : (half + 1) * HALF])
-
-        load_w(0, 2)
+        load_w(0, 1)
         load_scales(0)
-        load_wp(0, 0)
-        load_wp(0, 1)
-        load_w(2, 3)
-        load_wp(1, 0)
-        load_wp(1, 1)
+        nc.sync.dma_start(out=wp_raw[0][:], in_=wp_view[0])
+        load_w(1, 2)
+        nc.sync.dma_start(out=wp_raw[1][:], in_=wp_view[1])
         load_scales(1)
+        load_w(2, 3)
         load_w(3, 4)
+        load_scales(2)
         load_w(4, E)
 
-        gate_turned = psum.tile([P, PASSES * 2, C], F32, name="gate_turned", tag="bank3")
+        gate_turned = psum.tile([P, PER_ROW, C], F32, name="gate_turned", tag="bank7")
         for c in range(PER_ROW):
             nc.tensor.transpose(gate_turned[:, c, :], gate_rows[:, c * C : (c + 1) * C], ident[:])
-        nc.scalar.copy(out=gate_cols[:], in_=gate_turned[:, 0:PER_ROW, 0:GATE_ROWS])
+        nc.scalar.copy(out=gate_cols[:], in_=gate_turned[:, :, 0:GATE_ROWS])
 
         x_group = keep.tile([P, PACK * T], BF16, name="x_group", align_bytes=64)
-        for (a, b, share), raw in zip(X_CHUNKS, x_raw):
-            dst = x_group[:, PACK * a : PACK * b]
-            interleave(nc.scalar.copy, dst, raw, 0, share)
-            interleave(nc.vector.tensor_copy, dst, raw, share, b - a)
-            nc.vector.quantize_mx(out=x_codes[:, a:b].bitcast(FP8X4), scales=x_scales[:, a:b], in_=dst)
+        for a, cut, b in X_CHUNKS:
+            interleave(nc.scalar.copy, x_group[:], x_raw, cut, b)
+            interleave(nc.vector.tensor_copy, x_group[:], x_raw, a, cut)
+        for a, cut, b in X_CHUNKS:
+            nc.vector.quantize_mx(
+                out=x_codes[:, a:b].bitcast(FP8X4), scales=x_scales[:, a:b], in_=x_group[:, PACK * a : PACK * b]
+            )
 
         s_codes, s_scales, rows, c_groups, c_quant, wp_groups, wp_quant = {}, {}, {}, {}, {}, {}, {}
 
         def slots(a, b):
             return offsets[:, a * C // 16 : b * C // 16]
 
-        def gather(a, b, buffer=None):
+        def gather(a, b):
             codes = keep.tile([P, (b - a) * C], U32, name=f"s_codes{a}", align_bytes=64)
-            scales = keep.tile([P, (b - a) * C], U8, name=f"s_scales{a}", tag=buffer or f"s_scales{a}", align_bytes=64)
+            scales = keep.tile([P, (b - a) * C], U8, name=f"s_scales{a}", align_bytes=64)
             nc.vector.tensor_copy(codes[:], x_codes[:].indirect(slots(a, b)))
             nc.vector.tensor_copy(scales[:], x_scales[:].indirect(slots(a, b)))
             for e in range(a, b):
@@ -135,7 +125,7 @@ def tile_moe_nxt_lin_none_kernel(tc, xT, w_words, w_scales, wp, gate, offs, out)
         def gated_product(e):
             for g in range(PASSES):
                 rows[e, g] = keep.tile([P, PASS], BF16, name=f"c_rows{e}{g}", tag=f"rows{e}{g}", align_bytes=64)
-                y = psum.tile([P, PASS], F32, name=f"y{e}{g}", tag=f"bank{4 + 2 * (e % 2) + g}")
+                y = psum.tile([P, PASS], F32, name=f"y{e}{g}", tag=f"bank{2 * (e % 2) + g}")
                 nc.tensor.matmul_mx(
                     out=y[:],
                     lhsT=s_codes[e].bitcast(FP8X4),
@@ -152,71 +142,55 @@ def tile_moe_nxt_lin_none_kernel(tc, xT, w_words, w_scales, wp, gate, offs, out)
                     scale=gate_cols[:, e % PER_ROW, e // PER_ROW : e // PER_ROW + 1],
                 )
 
-        def turn(e, bank, unit=None):
-            unit = unit or (e, e + 1)
-            turned = psum.tile([P, PASSES, 2, C], F32, name=f"turned{e}", tag=f"bank{bank}")
+        def turn(e):
+            turned = psum.tile([P, PASSES, 2, C], F32, name=f"turned{e}", tag=f"bank{4 + e % 2}")
             for g in range(PASSES):
                 words = rows[e, g][:].bitcast(F32)
                 for u in range(2):
                     nc.tensor.transpose(turned[:, g, u, :], words[:, P * u : P * (u + 1)], ident[:])
-            if unit not in c_groups:
-                label = f"c_group{unit[0]}"
-                c_groups[unit] = keep.tile([P, unit[1] - unit[0], N], BF16, name=label, tag=label, align_bytes=64)
-            pairs = c_groups[unit][:, e - unit[0], :].bitcast(F32).rearrange("p (g s u) -> p g s u", g=PASSES, u=2)
+            c_groups[e] = keep.tile([P, N], BF16, name=f"c_group{e}", align_bytes=64)
+            pairs = c_groups[e][:].bitcast(F32).rearrange("p (g s u) -> p g s u", g=PASSES, u=2)
             nc.scalar.copy(out=pairs, in_=turned[:].rearrange("p g u s -> p g s u"))
 
-        def quantise_c(a, b):
-            codes = keep.tile([P, b - a, PASSES, C], U32, name=f"c_codes{a}", align_bytes=64)
-            scales = keep.tile([P, b - a, PASSES, C], U8, name=f"c_scales{a}", align_bytes=64)
+        def quantise_c(a):
+            codes = keep.tile([P, 1, PASSES, C], U32, name=f"c_codes{a}", align_bytes=64)
+            scales = keep.tile([P, 1, PASSES, C], U8, name=f"c_scales{a}", align_bytes=64)
             nc.vector.quantize_mx(
                 out=codes[:].rearrange("p e g s -> p (e g s)").bitcast(FP8X4),
                 scales=scales[:].rearrange("p e g s -> p (e g s)"),
-                in_=c_groups[a, b][:].rearrange("p e n -> p (e n)"),
+                in_=c_groups[a][:],
             )
-            for e in range(a, b):
-                c_quant[e] = (codes[:, e - a], scales[:, e - a])
+            c_quant[a] = (codes[:, 0], scales[:, 0])
 
-        def group_wp(a, b, g, copy, buffer=None):
-            if (a, b) not in wp_groups:
-                label = f"wp_group{a}"
-                wp_groups[a, b] = keep.tile(
-                    [P, b - a, PASSES, P * PACK], BF16, name=label, tag=buffer or label, align_bytes=64
-                )
-            at = (a % 2) * P
-            copy(
-                out=wp_groups[a, b][:, :, g, :].rearrange("p f (c i j) -> p f c j i", i=4, j=PACK),
-                in_=wp_raw[a // 2, g][:, :, at : at + (b - a) * P].rearrange("p j (f c i) -> p f c j i", f=b - a, i=4),
-            )
+        def group_wp(g, a, b, copy, buffer=None):
+            label = f"wp_group{g}{a}"
+            wp_groups[g, a] = keep.tile([P, (b - a) * P * PACK], BF16, name=label, tag=buffer or label, align_bytes=64)
+            interleave(copy, wp_groups[g, a][:], wp_raw[g][:, :, a * P : b * P], 0, (b - a) * P)
 
-        def quantise_wp(a, b):
-            codes = keep.tile([P, b - a, PASSES, P], U32, name=f"wp_codes{a}", align_bytes=64)
-            scales = keep.tile([P, b - a, PASSES, P], U8, name=f"wp_scales{a}", align_bytes=64)
-            nc.vector.quantize_mx(
-                out=codes[:].rearrange("p f g c -> p (f g c)").bitcast(FP8X4),
-                scales=scales[:].rearrange("p f g c -> p (f g c)"),
-                in_=wp_groups[a, b][:].rearrange("p f g c -> p (f g c)"),
-            )
+        def quantise_wp(g, a, b):
+            codes = keep.tile([P, (b - a) * P], U32, name=f"wp_codes{g}{a}", align_bytes=64)
+            scales = keep.tile([P, (b - a) * P], U8, name=f"wp_scales{g}{a}", align_bytes=64)
+            nc.vector.quantize_mx(out=codes[:].bitcast(FP8X4), scales=scales[:], in_=wp_groups[g, a][:])
             for f in range(a, b):
-                wp_quant[f] = (codes[:, f - a], scales[:, f - a])
+                wp_quant[f, g] = (codes[:, (f - a) * P : (f - a + 1) * P], scales[:, (f - a) * P : (f - a + 1) * P])
 
         windows = [keep.tile([P, T], F32, name=f"window{f}") for f in range(F_TILES)]
 
         def project(a, b, f_tiles, bank, buffer=None):
             width = (b - a) * C
             sums = psum.tile([P, 512], F32, name=f"sums{a}{f_tiles[0]}", tag=f"bank{bank}")
-            for i, f in enumerate(f_tiles):
-                for e in range(a, b):
-                    col = i * width + (e - a) * C
-                    for g in range(PASSES):
-                        nc.tensor.matmul_mx(
-                            out=sums[:, col : col + C],
-                            lhsT=wp_quant[f][0][:, g, :].bitcast(FP8X4),
-                            lhsT_scale=wp_quant[f][1][:, g, :],
-                            rhs=c_quant[e][0][:, g, :].bitcast(FP8X4),
-                            rhs_scale=c_quant[e][1][:, g, :],
-                            start=(g == 0),
-                            stop=(g == PASSES - 1),
-                        )
+            steps = [(g, i, f, e) for g in range(PASSES) for i, f in enumerate(f_tiles) for e in range(a, b)]
+            for step, (g, i, f, e) in enumerate(steps):
+                col = i * width + (e - a) * C
+                nc.tensor.matmul_mx(
+                    out=sums[:, col : col + C],
+                    lhsT=wp_quant[f, g][0].bitcast(FP8X4),
+                    lhsT_scale=wp_quant[f, g][1],
+                    rhs=c_quant[e][0][:, g, :].bitcast(FP8X4),
+                    rhs_scale=c_quant[e][1][:, g, :],
+                    start=(step == 0),
+                    stop=(step == len(steps) - 1),
+                )
             label = f"landed{a}{f_tiles[0]}"
             landed = keep.tile([P, len(f_tiles), width], F32, name=label, tag=buffer or label, align_bytes=64)
             nc.scalar.copy(out=landed[:].rearrange("p f s -> p (f s)"), in_=sums[:, : len(f_tiles) * width])
@@ -225,45 +199,42 @@ def tile_moe_nxt_lin_none_kernel(tc, xT, w_words, w_scales, wp, gate, offs, out)
                 if b == E:
                     nc.sync.dma_start(out=out[f * P : (f + 1) * P, :], in_=windows[f][:])
 
-        lower = (0, 1)
+        lower, upper = (0, 1), (2, 3)
 
         gather(0, 1)
         gated_product(0)
         gather(1, 3)
         gather(3, E)
-        turn(0, 0)
+        group_wp(0, 2, 4, nc.scalar.copy)
+        turn(0)
+        group_wp(0, 0, 2, nc.vector.tensor_copy)
+        quantise_c(0)
+        quantise_wp(0, 0, 2)
+        quantise_wp(0, 2, 4)
         gated_product(1)
-        turn(1, 1)
-        for g in range(PASSES):
-            for f in lower:
-                group_wp(f, f + 1, g, nc.vector.tensor_copy)
-        quantise_wp(0, 1)
-        quantise_c(0, 1)
-        quantise_wp(1, 2)
-        quantise_c(1, 2)
-        group_wp(2, 4, 0, nc.vector.tensor_copy, buffer="c_group1")
-        project(0, 1, (0,), 2)
-        project(0, 1, (1,), 3)
+        group_wp(1, 2, 4, nc.scalar.copy)
+        turn(1)
+        quantise_c(1)
+        for f in lower:
+            group_wp(1, f, f + 1, nc.vector.tensor_copy)
+        for f in lower:
+            quantise_wp(1, f, f + 1)
+        quantise_wp(1, 2, 4)
+        project(0, 1, (0,), 0)
+        project(0, 1, (1,), 1)
+        project(0, 1, upper, 6)
         gated_product(2)
-        turn(2, 0)
-        quantise_c(2, 3)
-        project(1, 2, lower, 2, buffer="rows21")
-        group_wp(2, 4, 1, nc.scalar.copy)
-        quantise_wp(2, 4)
-        project(2, 3, lower, 1, buffer="wp_raw11")
-        gated_product(3)
-        turn(3, 3)
-        quantise_c(3, 4)
-        project(0, 3, (2,), 7, buffer="rows31")
-        project(0, 3, (3,), 0)
-
-        gated_product(4)
-        turn(4, 2, (4, 6))
-        gated_product(5)
-        turn(5, 0, (4, 6))
-        quantise_c(4, 6)
-        project(3, 4, lower, 1, buffer="rows51")
-        project(4, 6, (0,), 3)
-        project(4, 6, (1,), 2)
-        project(3, 6, (2,), 0)
-        project(3, 6, (3,), 1)
+        project(1, 2, lower, 0)
+        for e in range(2, 5):
+            turn(e)
+            quantise_c(e)
+            project(e - 1, e, upper, 6 + (e + 1) % 2, buffer=f"rows{e}1")
+            gated_product(e + 1)
+            if e < 4:
+                project(e, e + 1, lower, 2 * ((e + 1) % 2))
+        turn(5)
+        quantise_c(5)
+        project(4, 5, lower, 2, buffer="rows51")
+        project(5, 6, lower, 0)
+        project(4, 6, (2,), 1)
+        project(4, 6, (3,), 3)

@@ -12,7 +12,7 @@ F_TILES = M // P
 GATE_ROWS = 2
 PER_ROW = E // GATE_ROWS
 SCALE_GROUP = 2
-X_CHUNKS = ((0, 352, 512), (512, 624, T))
+X_CHUNKS = ((0, 512, 192), (512, T, 128))
 
 FLOPS = 2 * K * N * E * C + 2 * N * M * T
 BYTES = 4 * K * T + E * K * N // 2 + E * (K // 32) * N + 4 * N * M + 4 * E * C + 2 * E * C + 4 * M * T
@@ -58,9 +58,12 @@ def tile_moe_nxt_lin_none_kernel(tc, xT, w_words, w_scales, wp, gate, offs, out)
         make_identity(nc, ident[:])
 
         x_view = xT.rearrange("(p j) t -> p j t", j=PACK)
-        x_raw = keep.tile([P, PACK, T], F32, name="x_raw")
+        x_raw = []
+        for a, b, share in X_CHUNKS:
+            raw = keep.tile([P, PACK, b - a], F32, name=f"x_raw{a}")
+            nc.sync.dma_start(out=raw[:], in_=x_view[:, :, a:b])
+            x_raw.append(raw)
         nc.sync.dma_start(offsets[:], offs)
-        nc.sync.dma_start(out=x_raw[:], in_=x_view)
         nc.sync.dma_start(out=gate_rows[0:GATE_ROWS, :], in_=gate[0:1, :].rearrange("o (r s) -> (o r) s", r=GATE_ROWS))
 
         w_codes = {}
@@ -100,13 +103,11 @@ def tile_moe_nxt_lin_none_kernel(tc, xT, w_words, w_scales, wp, gate, offs, out)
         nc.scalar.copy(out=gate_cols[:], in_=gate_turned[:, :, 0:GATE_ROWS])
 
         x_group = keep.tile([P, PACK * T], BF16, name="x_group", align_bytes=64)
-        for a, cut, b in X_CHUNKS:
-            interleave(nc.scalar.copy, x_group[:], x_raw, cut, b)
-            interleave(nc.vector.tensor_copy, x_group[:], x_raw, a, cut)
-        for a, cut, b in X_CHUNKS:
-            nc.vector.quantize_mx(
-                out=x_codes[:, a:b].bitcast(FP8X4), scales=x_scales[:, a:b], in_=x_group[:, PACK * a : PACK * b]
-            )
+        for (a, b, share), raw in zip(X_CHUNKS, x_raw):
+            dst = x_group[:, PACK * a : PACK * b]
+            interleave(nc.scalar.copy, dst, raw, 0, share)
+            interleave(nc.vector.tensor_copy, dst, raw, share, b - a)
+            nc.vector.quantize_mx(out=x_codes[:, a:b].bitcast(FP8X4), scales=x_scales[:, a:b], in_=dst)
 
         s_codes, s_scales, rows, c_groups, c_quant, wp_groups, wp_quant = {}, {}, {}, {}, {}, {}, {}
 

@@ -88,9 +88,9 @@ def tile_moe_nxt_lin_none_kernel(tc, xT, w_words, w_scales, wp, gate, offs, out)
 
         load_w(0, 1)
         load_scales(0)
-        nc.sync.dma_start(out=wp_raw[0][:], in_=wp_view[0])
         load_w(1, 2)
-        nc.sync.dma_start(out=wp_raw[1][:], in_=wp_view[1])
+        for g in range(PASSES):
+            nc.sync.dma_start(out=wp_raw[g][:], in_=wp_view[g])
         load_scales(1)
         load_w(2, 3)
         load_w(3, 4)
@@ -153,9 +153,9 @@ def tile_moe_nxt_lin_none_kernel(tc, xT, w_words, w_scales, wp, gate, offs, out)
             pairs = c_groups[e][:].bitcast(F32).rearrange("p (g s u) -> p g s u", g=PASSES, u=2)
             nc.scalar.copy(out=pairs, in_=turned[:].rearrange("p g u s -> p g s u"))
 
-        def quantise_c(a):
+        def quantise_c(a, buffer=None):
             codes = keep.tile([P, 1, PASSES, C], U32, name=f"c_codes{a}", align_bytes=64)
-            scales = keep.tile([P, 1, PASSES, C], U8, name=f"c_scales{a}", align_bytes=64)
+            scales = keep.tile([P, 1, PASSES, C], U8, name=f"c_scales{a}", tag=buffer or f"c_scales{a}", align_bytes=64)
             nc.vector.quantize_mx(
                 out=codes[:].rearrange("p e g s -> p (e g s)").bitcast(FP8X4),
                 scales=scales[:].rearrange("p e g s -> p (e g s)"),
@@ -163,14 +163,16 @@ def tile_moe_nxt_lin_none_kernel(tc, xT, w_words, w_scales, wp, gate, offs, out)
             )
             c_quant[a] = (codes[:, 0], scales[:, 0])
 
-        def group_wp(g, a, b, copy, buffer=None):
+        def group_wp(g, a, b, *copies):
             label = f"wp_group{g}{a}"
-            wp_groups[g, a] = keep.tile([P, (b - a) * P * PACK], BF16, name=label, tag=buffer or label, align_bytes=64)
-            interleave(copy, wp_groups[g, a][:], wp_raw[g][:, :, a * P : b * P], 0, (b - a) * P)
+            wp_groups[g, a] = keep.tile([P, (b - a) * P * PACK], BF16, name=label, align_bytes=64)
+            share = (b - a) * P // len(copies)
+            for i, copy in enumerate(copies):
+                interleave(copy, wp_groups[g, a][:], wp_raw[g][:, :, a * P : b * P], i * share, (i + 1) * share)
 
-        def quantise_wp(g, a, b):
+        def quantise_wp(g, a, b, buffer=None):
             codes = keep.tile([P, (b - a) * P], U32, name=f"wp_codes{g}{a}", align_bytes=64)
-            scales = keep.tile([P, (b - a) * P], U8, name=f"wp_scales{g}{a}", align_bytes=64)
+            scales = keep.tile([P, (b - a) * P], U8, name=f"wp_scales{g}{a}", tag=buffer or f"wp_scales{g}{a}", align_bytes=64)
             nc.vector.quantize_mx(out=codes[:].bitcast(FP8X4), scales=scales[:], in_=wp_groups[g, a][:])
             for f in range(a, b):
                 wp_quant[f, g] = (codes[:, (f - a) * P : (f - a + 1) * P], scales[:, (f - a) * P : (f - a + 1) * P])
@@ -206,30 +208,30 @@ def tile_moe_nxt_lin_none_kernel(tc, xT, w_words, w_scales, wp, gate, offs, out)
         gated_product(0)
         gather(1, 3)
         gather(3, E)
-        group_wp(0, 2, 4, nc.scalar.copy)
         turn(0)
+        gated_product(1)
+        turn(1)
+        group_wp(0, 2, 4, nc.scalar.copy)
         group_wp(0, 0, 2, nc.vector.tensor_copy)
         quantise_c(0)
         quantise_wp(0, 0, 2)
-        quantise_wp(0, 2, 4)
-        gated_product(1)
-        group_wp(1, 2, 4, nc.scalar.copy)
-        turn(1)
-        quantise_c(1)
         for f in lower:
             group_wp(1, f, f + 1, nc.vector.tensor_copy)
         for f in lower:
             quantise_wp(1, f, f + 1)
+        group_wp(1, 2, 4, nc.vector.tensor_copy, nc.scalar.copy)
+        quantise_c(1, buffer="wp_group10")
+        quantise_wp(0, 2, 4, buffer="wp_group11")
         quantise_wp(1, 2, 4)
         project(0, 1, (0,), 0)
         project(0, 1, (1,), 1)
         project(0, 1, upper, 6)
+        project(1, 2, lower, 7)
         gated_product(2)
-        project(1, 2, lower, 0)
         for e in range(2, 5):
             turn(e)
             quantise_c(e)
-            project(e - 1, e, upper, 6 + (e + 1) % 2, buffer=f"rows{e}1")
+            project(e - 1, e, upper, 0 if e == 2 else 6 + (e + 1) % 2, buffer=f"rows{e}1")
             gated_product(e + 1)
             if e < 4:
                 project(e, e + 1, lower, 2 * ((e + 1) % 2))

@@ -89,10 +89,10 @@ def tile_moe_nxt_lin_none_kernel(tc, xT, w_words, w_scales, wp, gate, offs, out)
         load_w(0, 1)
         load_scales(0)
         load_w(1, 2)
-        for g in range(PASSES):
-            nc.sync.dma_start(out=wp_raw[g][:], in_=wp_view[g])
+        nc.sync.dma_start(out=wp_raw[0][:], in_=wp_view[0])
         load_scales(1)
         load_w(2, 3)
+        nc.sync.dma_start(out=wp_raw[1][:], in_=wp_view[1])
         load_w(3, 4)
         load_scales(2)
         load_w(4, E)
@@ -143,8 +143,8 @@ def tile_moe_nxt_lin_none_kernel(tc, xT, w_words, w_scales, wp, gate, offs, out)
                     scale=gate_cols[:, e % PER_ROW, e // PER_ROW : e // PER_ROW + 1],
                 )
 
-        def turn(e):
-            turned = psum.tile([P, PASSES, 2, C], F32, name=f"turned{e}", tag=f"bank{4 + e % 2}")
+        def turn(e, bank):
+            turned = psum.tile([P, PASSES, 2, C], F32, name=f"turned{e}", tag=f"bank{bank}")
             for g in range(PASSES):
                 words = rows[e, g][:].bitcast(F32)
                 for u in range(2):
@@ -179,65 +179,83 @@ def tile_moe_nxt_lin_none_kernel(tc, xT, w_words, w_scales, wp, gate, offs, out)
 
         windows = [keep.tile([P, T], F32, name=f"window{f}") for f in range(F_TILES)]
 
-        def project(a, b, f_tiles, bank, buffer=None):
-            width = (b - a) * C
-            sums = psum.tile([P, 512], F32, name=f"sums{a}{f_tiles[0]}", tag=f"bank{bank}")
-            steps = [(g, i, f, e) for g in range(PASSES) for i, f in enumerate(f_tiles) for e in range(a, b)]
-            for step, (g, i, f, e) in enumerate(steps):
-                col = i * width + (e - a) * C
-                nc.tensor.matmul_mx(
-                    out=sums[:, col : col + C],
-                    lhsT=wp_quant[f, g][0].bitcast(FP8X4),
-                    lhsT_scale=wp_quant[f, g][1],
-                    rhs=c_quant[e][0][:, g, :].bitcast(FP8X4),
-                    rhs_scale=c_quant[e][1][:, g, :],
-                    start=(step == 0),
-                    stop=(step == len(steps) - 1),
-                )
-            label = f"landed{a}{f_tiles[0]}"
-            landed = keep.tile([P, len(f_tiles), width], F32, name=label, tag=buffer or label, align_bytes=64)
-            nc.scalar.copy(out=landed[:].rearrange("p f s -> p (f s)"), in_=sums[:, : len(f_tiles) * width])
-            for i, f in enumerate(f_tiles):
-                nc.vector.tensor_copy(windows[f][:].indirect(slots(a, b)), landed[:, i, :])
-                if b == E:
-                    nc.sync.dma_start(out=out[f * P : (f + 1) * P, :], in_=windows[f][:])
+        def project(bank, *parts):
+            sums = psum.tile([P, 512], F32, name=f"sums{parts[0][0]}{parts[0][1]}", tag=f"bank{bank}")
+            views, steps, col = {}, [], 0
+            for f, a, b in parts:
+                views[f, a] = sums[:, col : col + (b - a) * C]
+                steps.extend((f, e, col + (e - a) * C) for e in reversed(range(a, b)))
+                col += (b - a) * C
+            for g in range(PASSES):
+                for i, (f, e, first) in enumerate(steps):
+                    nc.tensor.matmul_mx(
+                        out=sums[:, first : first + C],
+                        lhsT=wp_quant[f, g][0].bitcast(FP8X4),
+                        lhsT_scale=wp_quant[f, g][1],
+                        rhs=c_quant[e][0][:, g, :].bitcast(FP8X4),
+                        rhs_scale=c_quant[e][1][:, g, :],
+                        start=(g == 0 and i == 0),
+                        stop=(g == PASSES - 1 and i == len(steps) - 1),
+                    )
+            out_sums.update(views)
 
-        lower, upper = (0, 1), (2, 3)
+        def land(copy, f, a, b):
+            tile = keep.tile([P, (b - a) * C], F32, name=f"landed{f}{a}", align_bytes=64)
+            copy(out=tile[:], in_=out_sums[f, a])
+            for e in range(a, b):
+                landed[f, e] = (tile, (e - a) * C)
+
+        def scatter(on_vector, f, a, b):
+            tile, first = landed[f, a]
+            values = tile[:, first : first + (b - a) * C]
+            if on_vector:
+                nc.vector.tensor_copy(windows[f][:].indirect(slots(a, b)), values)
+            else:
+                nc.scalar.activation(out=windows[f][:].indirect(slots(a, b)), in_=values, func=COPY)
+            if b == E:
+                nc.sync.dma_start(out=out[f * P : (f + 1) * P, :], in_=windows[f][:])
+
+        out_sums, landed = {}, {}
+        vector, scalar = nc.vector.tensor_copy, nc.scalar.copy
 
         gather(0, 1)
         gated_product(0)
         gather(1, 3)
         gather(3, E)
-        turn(0)
-        gated_product(1)
-        turn(1)
-        group_wp(0, 2, 4, nc.scalar.copy)
-        group_wp(0, 0, 2, nc.vector.tensor_copy)
-        quantise_c(0)
-        quantise_wp(0, 0, 2)
-        for f in lower:
-            group_wp(1, f, f + 1, nc.vector.tensor_copy)
-        for f in lower:
-            quantise_wp(1, f, f + 1)
-        group_wp(1, 2, 4, nc.vector.tensor_copy, nc.scalar.copy)
-        quantise_c(1, buffer="wp_group10")
-        quantise_wp(0, 2, 4, buffer="wp_group11")
-        quantise_wp(1, 2, 4)
-        project(0, 1, (0,), 0)
-        project(0, 1, (1,), 1)
-        project(0, 1, upper, 6)
-        project(1, 2, lower, 7)
-        gated_product(2)
-        for e in range(2, 5):
-            turn(e)
-            quantise_c(e)
-            project(e - 1, e, upper, 0 if e == 2 else 6 + (e + 1) % 2, buffer=f"rows{e}1")
-            gated_product(e + 1)
-            if e < 4:
-                project(e, e + 1, lower, 2 * ((e + 1) % 2))
-        turn(5)
+        for e in range(E):
+            if e + 1 < E:
+                gated_product(e + 1)
+            turn(e, 2 * ((e + 1) % 2) if e + 1 < E else 4)
+        for g in range(PASSES):
+            group_wp(g, 0, 2, vector)
+            group_wp(g, 2, 4, vector)
+            quantise_c(2 * g, buffer="wp_raw1" if g else None)
+            quantise_wp(g, 0, 2)
+            quantise_wp(g, 2, 4)
+            quantise_c(2 * g + 1)
+        project(1, (0, 0, 3))
+        land(vector, 0, 0, 3)
+        scatter(True, 0, 0, 3)
+        quantise_c(4)
         quantise_c(5)
-        project(4, 5, lower, 2, buffer="rows51")
-        project(5, 6, lower, 0)
-        project(4, 6, (2,), 1)
-        project(4, 6, (3,), 3)
+        project(3, (3, 0, 3))
+        project(2, (1, 0, 3))
+        project(4, (2, 0, 3))
+        project(5, (0, 3, E))
+        project(6, (2, 3, E))
+        project(7, (1, 3, E))
+        project(0, (3, 3, E))
+        land(scalar, 3, 0, 3)
+        scatter(False, 3, 0, 3)
+        land(vector, 1, 0, 3)
+        land(vector, 0, 3, E)
+        land(scalar, 2, 0, 3)
+        land(scalar, 2, 3, E)
+        scatter(True, 1, 0, 3)
+        scatter(False, 2, 0, 3)
+        land(vector, 1, 3, E)
+        land(scalar, 3, 3, E)
+        scatter(True, 0, 3, E)
+        scatter(False, 2, 3, E)
+        scatter(True, 1, 3, E)
+        scatter(False, 3, 3, E)

@@ -11,8 +11,8 @@ PASSES = N // PASS
 F_TILES = M // P
 GATE_ROWS = 2
 PER_ROW = E // GATE_ROWS
-SCALE_GROUP = 2
-X_CHUNKS = ((0, 512, 192), (512, T, 128))
+SCALE_GROUPS = ((0, 2), (2, E))
+X_CHUNKS = ((0, 256, 128), (256, 512, 128), (512, T, 96))
 
 FLOPS = 2 * K * N * E * C + 2 * N * M * T
 BYTES = 4 * K * T + E * K * N // 2 + E * (K // 32) * N + 4 * N * M + 4 * E * C + 2 * E * C + 4 * M * T
@@ -25,6 +25,7 @@ U16 = mybir.dt.uint16
 U8 = mybir.dt.uint8
 FP8X4 = mybir.dt.float8_e4m3fn_x4
 FP4X4 = mybir.dt.float4_e2m1fn_x4
+MULT = mybir.AluOpType.mult
 COPY = mybir.ActivationFunctionType.Copy
 
 
@@ -39,6 +40,7 @@ def tile_moe_nxt_lin_none_kernel(tc, xT, w_words, w_scales, wp, gate, offs, out)
     nc = tc.nc
     with ExitStack() as ctx:
         keep = ctx.enter_context(tc.tile_pool(name="keep", bufs=1))
+        reuse = ctx.enter_context(tc.tile_pool(name="reuse", bufs=1))
         psum = ctx.enter_context(tc.psum_pool(name="psum", bufs=1))
 
         offsets = keep.tile([P, E * C // 16], U16, name="offsets")
@@ -47,9 +49,8 @@ def tile_moe_nxt_lin_none_kernel(tc, xT, w_words, w_scales, wp, gate, offs, out)
         ident = keep.tile([P, P], F32, name="ident")
         x_codes = keep.tile([P, T], U32, name="x_codes", align_bytes=64)
         x_scales = keep.tile([P, T], U8, name="x_scales", align_bytes=64)
-        w_scale_tiles = [
-            keep.tile([P, SCALE_GROUP, N], U8, name=f"w_scales{i}", align_bytes=64) for i in range(E // SCALE_GROUP)
-        ]
+        w_scale_tiles = [keep.tile([P, b - a, N], U8, name=f"w_scales{a}", align_bytes=64) for a, b in SCALE_GROUPS]
+        w_planes = [tile[:, e, :] for tile, (a, b) in zip(w_scale_tiles, SCALE_GROUPS) for e in range(b - a)]
 
         nc.gpsimd.memset(gate_rows[:], 0.0)
         for tile in w_scale_tiles:
@@ -63,8 +64,11 @@ def tile_moe_nxt_lin_none_kernel(tc, xT, w_words, w_scales, wp, gate, offs, out)
             raw = keep.tile([P, PACK, b - a], F32, name=f"x_raw{a}")
             nc.sync.dma_start(out=raw[:], in_=x_view[:, :, a:b])
             x_raw.append(raw)
-        nc.sync.dma_start(offsets[:], offs)
-        nc.sync.dma_start(out=gate_rows[0:GATE_ROWS, :], in_=gate[0:1, :].rearrange("o (r s) -> (o r) s", r=GATE_ROWS))
+            if a == 0:
+                nc.sync.dma_start(offsets[:], offs)
+                nc.sync.dma_start(
+                    out=gate_rows[0:GATE_ROWS, :], in_=gate[0:1, :].rearrange("o (r s) -> (o r) s", r=GATE_ROWS)
+                )
 
         w_codes = {}
 
@@ -80,21 +84,29 @@ def tile_moe_nxt_lin_none_kernel(tc, xT, w_words, w_scales, wp, gate, offs, out)
             for r in range(4):
                 nc.sync.dma_start(
                     out=w_scale_tiles[i][r:P:32, :, :].bitcast(I32),
-                    in_=scale_rows[r, :, i * SCALE_GROUP : (i + 1) * SCALE_GROUP, :],
+                    in_=scale_rows[r, :, SCALE_GROUPS[i][0] : SCALE_GROUPS[i][1], :],
                 )
 
         wp_view = wp.rearrange("(g p j) f -> g p j f", p=P, j=PACK)
-        wp_raw = [keep.tile([P, PACK, M], F32, name=f"wp_raw{g}", align_bytes=64) for g in range(PASSES)]
+        wp_raw = {}
 
+        def load_wp(g, a, b):
+            if g == 0:
+                raw = keep.tile([P, PACK, (b - a) * P], F32, name=f"wp_raw{g}{a}", align_bytes=64)
+            else:
+                raw = reuse.tile([P, PACK, (b - a) * P], F32, name=f"wp_raw{g}{a}", align_bytes=64, offset=0)
+            nc.sync.dma_start(out=raw[:], in_=wp_view[g][:, :, a * P : b * P])
+            for f in range(a, b, 2):
+                wp_raw[g, f] = raw[:, :, (f - a) * P : (f - a + 2) * P]
+
+        load_wp(0, 0, 2)
         load_w(0, 1)
         load_scales(0)
         load_w(1, 2)
-        nc.sync.dma_start(out=wp_raw[0][:], in_=wp_view[0])
+        load_wp(0, 2, 4)
         load_scales(1)
-        load_w(2, 3)
-        nc.sync.dma_start(out=wp_raw[1][:], in_=wp_view[1])
-        load_w(3, 4)
-        load_scales(2)
+        load_w(2, 4)
+        load_wp(1, 0, 4)
         load_w(4, E)
 
         gate_turned = psum.tile([P, PER_ROW, C], F32, name="gate_turned", tag="bank7")
@@ -123,39 +135,50 @@ def tile_moe_nxt_lin_none_kernel(tc, xT, w_words, w_scales, wp, gate, offs, out)
                 s_codes[e] = codes[:, (e - a) * C : (e - a + 1) * C]
                 s_scales[e] = scales[:, (e - a) * C : (e - a + 1) * C]
 
-        def gated_product(e):
+        def gated_product(e, banks, on_vector=()):
             for g in range(PASSES):
-                rows[e, g] = keep.tile([P, PASS], BF16, name=f"c_rows{e}{g}", tag=f"rows{e}{g}", align_bytes=64)
-                y = psum.tile([P, PASS], F32, name=f"y{e}{g}", tag=f"bank{2 * (e % 2) + g}")
+                if e >= 4 and g == 1:
+                    place = 8 * N + (e - 4) * N
+                    rows[e, g] = reuse.tile([P, PASS], BF16, name=f"c_rows{e}{g}", align_bytes=64, offset=place)
+                else:
+                    rows[e, g] = keep.tile([P, PASS], BF16, name=f"c_rows{e}{g}", align_bytes=64)
+                y = psum.tile([P, PASS], F32, name=f"y{e}{g}", tag=f"bank{banks[g]}")
                 nc.tensor.matmul_mx(
                     out=y[:],
                     lhsT=s_codes[e].bitcast(FP8X4),
                     lhsT_scale=s_scales[e],
                     rhs=w_codes[e][:, 2 * PASS * g : 2 * PASS * (g + 1)].bitcast(FP4X4),
-                    rhs_scale=w_scale_tiles[e // SCALE_GROUP][:, e % SCALE_GROUP, PASS * g : PASS * (g + 1)],
+                    rhs_scale=w_planes[e][:, PASS * g : PASS * (g + 1)],
                     start=True,
                     stop=True,
                 )
-                nc.scalar.activation(
-                    out=rows[e, g][:].rearrange("s (u p i) -> s u p i", u=2, i=2),
-                    in_=y[:].rearrange("s (p u i) -> s u p i", u=2, i=2),
-                    func=COPY,
-                    scale=gate_cols[:, e % PER_ROW, e // PER_ROW : e // PER_ROW + 1],
-                )
+                rounded = rows[e, g][:].rearrange("s (u p i) -> s u p i", u=2, i=2)
+                sums = y[:].rearrange("s (p u i) -> s u p i", u=2, i=2)
+                weight = gate_cols[:, e % PER_ROW, e // PER_ROW : e // PER_ROW + 1]
+                if g in on_vector:
+                    nc.vector.tensor_scalar(out=rounded, in0=sums, scalar1=weight, scalar2=None, op0=MULT)
+                else:
+                    nc.scalar.activation(out=rounded, in_=sums, func=COPY, scale=weight)
 
-        def turn(e, bank):
+        def turn(e, bank, copy, offset=None):
             turned = psum.tile([P, PASSES, 2, C], F32, name=f"turned{e}", tag=f"bank{bank}")
             for g in range(PASSES):
                 words = rows[e, g][:].bitcast(F32)
                 for u in range(2):
                     nc.tensor.transpose(turned[:, g, u, :], words[:, P * u : P * (u + 1)], ident[:])
-            c_groups[e] = keep.tile([P, N], BF16, name=f"c_group{e}", align_bytes=64)
+            if offset is None:
+                c_groups[e] = keep.tile([P, N], BF16, name=f"c_group{e}", align_bytes=64)
+            else:
+                c_groups[e] = reuse.tile([P, N], BF16, name=f"c_group{e}", align_bytes=64, offset=offset)
             pairs = c_groups[e][:].bitcast(F32).rearrange("p (g s u) -> p g s u", g=PASSES, u=2)
-            nc.scalar.copy(out=pairs, in_=turned[:].rearrange("p g u s -> p g s u"))
+            copy(out=pairs, in_=turned[:].rearrange("p g u s -> p g s u"))
 
-        def quantise_c(a, buffer=None):
+        def quantise_c(a, offset=None):
             codes = keep.tile([P, 1, PASSES, C], U32, name=f"c_codes{a}", align_bytes=64)
-            scales = keep.tile([P, 1, PASSES, C], U8, name=f"c_scales{a}", tag=buffer or f"c_scales{a}", align_bytes=64)
+            if offset is None:
+                scales = keep.tile([P, 1, PASSES, C], U8, name=f"c_scales{a}", align_bytes=64)
+            else:
+                scales = reuse.tile([P, 1, PASSES, C], U8, name=f"c_scales{a}", align_bytes=64, offset=offset)
             nc.vector.quantize_mx(
                 out=codes[:].rearrange("p e g s -> p (e g s)").bitcast(FP8X4),
                 scales=scales[:].rearrange("p e g s -> p (e g s)"),
@@ -168,7 +191,7 @@ def tile_moe_nxt_lin_none_kernel(tc, xT, w_words, w_scales, wp, gate, offs, out)
             wp_groups[g, a] = keep.tile([P, (b - a) * P * PACK], BF16, name=label, align_bytes=64)
             share = (b - a) * P // len(copies)
             for i, copy in enumerate(copies):
-                interleave(copy, wp_groups[g, a][:], wp_raw[g][:, :, a * P : b * P], i * share, (i + 1) * share)
+                interleave(copy, wp_groups[g, a][:], wp_raw[g, a], i * share, (i + 1) * share)
 
         def quantise_wp(g, a, b, buffer=None):
             codes = keep.tile([P, (b - a) * P], U32, name=f"wp_codes{g}{a}", align_bytes=64)
@@ -177,13 +200,13 @@ def tile_moe_nxt_lin_none_kernel(tc, xT, w_words, w_scales, wp, gate, offs, out)
             for f in range(a, b):
                 wp_quant[f, g] = (codes[:, (f - a) * P : (f - a + 1) * P], scales[:, (f - a) * P : (f - a + 1) * P])
 
-        windows = [keep.tile([P, T], F32, name=f"window{f}") for f in range(F_TILES)]
+        windows = [keep.tile([P, T], F32, name=f"window{f}") for f in range(F_TILES - 1)]
+        windows.append(reuse.tile([P, T], F32, name="window3", align_bytes=64, offset=8 * N))
 
         def project(bank, *parts):
             sums = psum.tile([P, 512], F32, name=f"sums{parts[0][0]}{parts[0][1]}", tag=f"bank{bank}")
-            views, steps, col = {}, [], 0
+            steps, col = [], 0
             for f, a, b in parts:
-                views[f, a] = sums[:, col : col + (b - a) * C]
                 steps.extend((f, e, col + (e - a) * C) for e in reversed(range(a, b)))
                 col += (b - a) * C
             for g in range(PASSES):
@@ -197,13 +220,15 @@ def tile_moe_nxt_lin_none_kernel(tc, xT, w_words, w_scales, wp, gate, offs, out)
                         start=(g == 0 and i == 0),
                         stop=(g == PASSES - 1 and i == len(steps) - 1),
                     )
-            out_sums.update(views)
+            return sums, steps
 
-        def land(copy, f, a, b):
-            tile = keep.tile([P, (b - a) * C], F32, name=f"landed{f}{a}", align_bytes=64)
-            copy(out=tile[:], in_=out_sums[f, a])
-            for e in range(a, b):
-                landed[f, e] = (tile, (e - a) * C)
+        def land(copy, sums, buffer=None):
+            bank, places = sums
+            label = "landed%d%d" % places[0][:2]
+            tile = keep.tile([P, len(places) * C], F32, name=label, tag=buffer or label, align_bytes=64)
+            copy(out=tile[:], in_=bank[:, : len(places) * C])
+            for f, e, first in places:
+                landed[f, e] = (tile, first)
 
         def scatter(on_vector, f, a, b):
             tile, first = landed[f, a]
@@ -213,48 +238,54 @@ def tile_moe_nxt_lin_none_kernel(tc, xT, w_words, w_scales, wp, gate, offs, out)
             else:
                 nc.scalar.activation(out=windows[f][:].indirect(slots(a, b)), in_=values, func=COPY)
             if b == E:
-                nc.sync.dma_start(out=out[f * P : (f + 1) * P, :], in_=windows[f][:])
+                queue = nc.sync if on_vector else nc.scalar
+                queue.dma_start(out=out[f * P : (f + 1) * P, :], in_=windows[f][:])
 
-        out_sums, landed = {}, {}
+        landed = {}
         vector, scalar = nc.vector.tensor_copy, nc.scalar.copy
 
+        group_wp(0, 0, 2, scalar)
         gather(0, 1)
-        gated_product(0)
+        gated_product(0, (0, 1))
         gather(1, 3)
         gather(3, E)
-        for e in range(E):
-            if e + 1 < E:
-                gated_product(e + 1)
-            turn(e, 2 * ((e + 1) % 2) if e + 1 < E else 4)
-        for g in range(PASSES):
-            group_wp(g, 0, 2, vector)
-            group_wp(g, 2, 4, vector)
-            quantise_c(2 * g, buffer="wp_raw1" if g else None)
-            quantise_wp(g, 0, 2)
-            quantise_wp(g, 2, 4)
-            quantise_c(2 * g + 1)
-        project(1, (0, 0, 3))
-        land(vector, 0, 0, 3)
+        gated_product(1, (2, 3))
+        turn(0, 4, scalar)
+        turn(1, 5, scalar)
+        group_wp(0, 2, 4, vector)
+        quantise_wp(0, 0, 2)
+        quantise_wp(0, 2, 4)
+        quantise_c(0)
+        quantise_c(1)
+        group_wp(1, 0, 2, vector)
+        group_wp(1, 2, 4, vector)
+        quantise_wp(1, 0, 2)
+        quantise_wp(1, 2, 4)
+        gated_product(2, (0, 1))
+        gated_product(3, (2, 3))
+        turn(2, 4, scalar)
+        turn(3, 5, scalar)
+        gated_product(5, (2, 3), on_vector=(0, 1))
+        quantise_c(2, offset=0)
+        gated_product(4, (0, 1), on_vector=(1,))
+        quantise_c(3, offset=2 * N)
+        turn(5, 4, scalar)
+        turn(4, 5, scalar)
+        land(scalar, project(6, (3, 0, 3)))
+        first = project(7, (0, 0, 3))
+        land(vector, first)
         scatter(True, 0, 0, 3)
+        scatter(False, 3, 0, 3)
         quantise_c(4)
         quantise_c(5)
-        project(3, (3, 0, 3))
-        project(2, (1, 0, 3))
-        project(4, (2, 0, 3))
-        project(5, (0, 3, E))
-        project(6, (2, 3, E))
-        project(7, (1, 3, E))
-        project(0, (3, 3, E))
-        land(scalar, 3, 0, 3)
-        scatter(False, 3, 0, 3)
-        land(vector, 1, 0, 3)
-        land(vector, 0, 3, E)
-        land(scalar, 2, 0, 3)
-        land(scalar, 2, 3, E)
+        land(vector, project(7, (1, 0, 3)))
+        land(scalar, project(6, (2, 0, 3)))
+        land(vector, project(0, (0, 3, E)))
+        land(scalar, project(1, (2, 3, E)))
         scatter(True, 1, 0, 3)
         scatter(False, 2, 0, 3)
-        land(vector, 1, 3, E)
-        land(scalar, 3, 3, E)
+        land(vector, project(2, (1, 3, E)))
+        land(scalar, project(3, (3, 3, E)))
         scatter(True, 0, 3, E)
         scatter(False, 2, 3, E)
         scatter(True, 1, 3, E)

@@ -12,7 +12,7 @@ F_TILES = M // P
 GATE_ROWS = 2
 PER_ROW = E // GATE_ROWS
 SCALE_GROUPS = ((0, 2), (2, E))
-X_CHUNKS = ((0, 256, 128), (256, 512, 128), (512, T, 96))
+X_CHUNKS = ((0, 512, 208), (512, T, 128))
 
 FLOPS = 2 * K * N * E * C + 2 * N * M * T
 BYTES = 4 * K * T + E * K * N // 2 + E * (K // 32) * N + 4 * N * M + 4 * E * C + 2 * E * C + 4 * M * T
@@ -103,11 +103,11 @@ def tile_moe_nxt_lin_none_kernel(tc, xT, w_words, w_scales, wp, gate, offs, out)
         load_w(0, 1)
         load_scales(0)
         load_w(1, 2)
-        load_wp(0, 2, 4)
         load_scales(1)
-        load_w(2, 4)
+        for e in range(2, E):
+            load_w(e, e + 1)
+        load_wp(0, 2, 4)
         load_wp(1, 0, 4)
-        load_w(4, E)
 
         gate_turned = psum.tile([P, PER_ROW, C], F32, name="gate_turned", tag="bank7")
         for c in range(PER_ROW):
@@ -137,11 +137,7 @@ def tile_moe_nxt_lin_none_kernel(tc, xT, w_words, w_scales, wp, gate, offs, out)
 
         def gated_product(e, banks, on_vector=()):
             for g in range(PASSES):
-                if e >= 4 and g == 1:
-                    place = 8 * N + (e - 4) * N
-                    rows[e, g] = reuse.tile([P, PASS], BF16, name=f"c_rows{e}{g}", align_bytes=64, offset=place)
-                else:
-                    rows[e, g] = keep.tile([P, PASS], BF16, name=f"c_rows{e}{g}", align_bytes=64)
+                rows[e, g] = keep.tile([P, PASS], BF16, name=f"c_rows{e}{g}", align_bytes=64)
                 y = psum.tile([P, PASS], F32, name=f"y{e}{g}", tag=f"bank{banks[g]}")
                 nc.tensor.matmul_mx(
                     out=y[:],
@@ -173,12 +169,9 @@ def tile_moe_nxt_lin_none_kernel(tc, xT, w_words, w_scales, wp, gate, offs, out)
             pairs = c_groups[e][:].bitcast(F32).rearrange("p (g s u) -> p g s u", g=PASSES, u=2)
             copy(out=pairs, in_=turned[:].rearrange("p g u s -> p g s u"))
 
-        def quantise_c(a, offset=None):
+        def quantise_c(a, buffer=None):
             codes = keep.tile([P, 1, PASSES, C], U32, name=f"c_codes{a}", align_bytes=64)
-            if offset is None:
-                scales = keep.tile([P, 1, PASSES, C], U8, name=f"c_scales{a}", align_bytes=64)
-            else:
-                scales = reuse.tile([P, 1, PASSES, C], U8, name=f"c_scales{a}", align_bytes=64, offset=offset)
+            scales = keep.tile([P, 1, PASSES, C], U8, name=f"c_scales{a}", tag=buffer or f"c_scales{a}", align_bytes=64)
             nc.vector.quantize_mx(
                 out=codes[:].rearrange("p e g s -> p (e g s)").bitcast(FP8X4),
                 scales=scales[:].rearrange("p e g s -> p (e g s)"),
@@ -200,8 +193,7 @@ def tile_moe_nxt_lin_none_kernel(tc, xT, w_words, w_scales, wp, gate, offs, out)
             for f in range(a, b):
                 wp_quant[f, g] = (codes[:, (f - a) * P : (f - a + 1) * P], scales[:, (f - a) * P : (f - a + 1) * P])
 
-        windows = [keep.tile([P, T], F32, name=f"window{f}") for f in range(F_TILES - 1)]
-        windows.append(reuse.tile([P, T], F32, name="window3", align_bytes=64, offset=8 * N))
+        windows = [keep.tile([P, T], F32, name=f"window{f}") for f in range(F_TILES)]
 
         def project(bank, *parts):
             sums = psum.tile([P, 512], F32, name=f"sums{parts[0][0]}{parts[0][1]}", tag=f"bank{bank}")
@@ -222,10 +214,13 @@ def tile_moe_nxt_lin_none_kernel(tc, xT, w_words, w_scales, wp, gate, offs, out)
                     )
             return sums, steps
 
-        def land(copy, sums, buffer=None):
+        def land(copy, sums, offset=None):
             bank, places = sums
             label = "landed%d%d" % places[0][:2]
-            tile = keep.tile([P, len(places) * C], F32, name=label, tag=buffer or label, align_bytes=64)
+            if offset is None:
+                tile = keep.tile([P, len(places) * C], F32, name=label, align_bytes=64)
+            else:
+                tile = reuse.tile([P, len(places) * C], F32, name=label, align_bytes=64, offset=offset)
             copy(out=tile[:], in_=bank[:, : len(places) * C])
             for f, e, first in places:
                 landed[f, e] = (tile, first)
@@ -250,42 +245,34 @@ def tile_moe_nxt_lin_none_kernel(tc, xT, w_words, w_scales, wp, gate, offs, out)
         gather(1, 3)
         gather(3, E)
         gated_product(1, (2, 3))
-        turn(0, 4, scalar)
-        turn(1, 5, scalar)
-        group_wp(0, 2, 4, vector)
         quantise_wp(0, 0, 2)
+        for e in range(4):
+            turn(e, 4 + e % 2, scalar)
+            gated_product(e + 2, (2 * (e % 2), 2 * (e % 2) + 1), on_vector=(1,))
+            quantise_c(e)
+        group_wp(0, 2, 4, vector)
         quantise_wp(0, 2, 4)
-        quantise_c(0)
-        quantise_c(1)
         group_wp(1, 0, 2, vector)
-        group_wp(1, 2, 4, vector)
+        group_wp(1, 2, 4, scalar)
         quantise_wp(1, 0, 2)
         quantise_wp(1, 2, 4)
-        gated_product(2, (0, 1))
-        gated_product(3, (2, 3))
-        turn(2, 4, scalar)
-        turn(3, 5, scalar)
-        gated_product(5, (2, 3), on_vector=(0, 1))
-        quantise_c(2, offset=0)
-        gated_product(4, (0, 1), on_vector=(1,))
-        quantise_c(3, offset=2 * N)
-        turn(5, 4, scalar)
-        turn(4, 5, scalar)
-        land(scalar, project(6, (3, 0, 3)))
-        first = project(7, (0, 0, 3))
-        land(vector, first)
-        scatter(True, 0, 0, 3)
-        scatter(False, 3, 0, 3)
+        turn(4, 4, scalar, offset=0)
+        turn(5, 5, scalar, offset=2 * N)
+        early = [project(bank, (f, 0, 3)) for f, bank in ((0, 6), (2, 0), (1, 7), (3, 1))]
         quantise_c(4)
+        land(vector, early[0])
+        land(vector, early[2])
         quantise_c(5)
-        land(vector, project(7, (1, 0, 3)))
-        land(scalar, project(6, (2, 0, 3)))
-        land(vector, project(0, (0, 3, E)))
-        land(scalar, project(1, (2, 3, E)))
-        scatter(True, 1, 0, 3)
+        land(scalar, early[1])
+        land(scalar, early[3])
+        scatter(True, 0, 0, 3)
         scatter(False, 2, 0, 3)
-        land(vector, project(2, (1, 3, E)))
-        land(scalar, project(3, (3, 3, E)))
+        land(vector, project(2, (0, 3, E)))
+        land(scalar, project(3, (2, 3, E)))
+        scatter(True, 1, 0, 3)
+        scatter(False, 3, 0, 3)
+        land(vector, project(4, (1, 3, E)))
+        land(scalar, project(5, (3, 3, E)))
         scatter(True, 0, 3, E)
         scatter(False, 2, 3, E)
         scatter(True, 1, 3, E)

@@ -267,13 +267,14 @@ def tile_moe_nxt_lin_none_kernel(tc, xT, w_words, w_scales, wp, gate, offs, out)
         land(scalar, early[3])
         scatter(True, 0, 0, 3)
         scatter(False, 2, 0, 3)
-        land(vector, project(2, (0, 3, E)))
-        land(scalar, project(3, (2, 3, E)))
+        land(vector, project(2, (0, 3, E), (2, 5, E)))
+        land(scalar, project(3, (2, 3, 5)))
         scatter(True, 1, 0, 3)
         scatter(False, 3, 0, 3)
         land(vector, project(4, (1, 3, E)))
         land(scalar, project(5, (3, 3, E)))
+        scatter(False, 2, 3, 5)
         scatter(True, 0, 3, E)
-        scatter(False, 2, 3, E)
+        scatter(True, 2, 5, E)
         scatter(True, 1, 3, E)
         scatter(False, 3, 3, E)

@@ -100,12 +100,11 @@ def tile_moe_nxt_lin_none_kernel(tc, xT, w_words, w_scales, wp, gate, offs, out)
                 wp_raw[g, f] = raw[:, :, (f - a) * P : (f - a + 2) * P]
 
         load_wp(0, 0, 2)
-        load_w(0, 1)
+        load_w(0, 2)
         load_scales(0)
-        load_w(1, 2)
+        load_w(2, 4)
         load_scales(1)
-        for e in range(2, E):
-            load_w(e, e + 1)
+        load_w(4, E)
         load_wp(0, 2, 4)
         load_wp(1, 0, 4)
 

@@ -100,12 +100,13 @@ def tile_moe_nxt_lin_none_kernel(tc, xT, w_words, w_scales, wp, gate, offs, out)
                 wp_raw[g, f] = raw[:, :, (f - a) * P : (f - a + 2) * P]
 
         load_wp(0, 0, 2)
-        load_w(0, 2)
+        load_w(0, 1)
         load_scales(0)
+        load_w(1, 2)
         load_w(2, 4)
         load_scales(1)
-        load_w(4, E)
         load_wp(0, 2, 4)
+        load_w(4, E)
         load_wp(1, 0, 4)
 
         gate_turned = psum.tile([P, PER_ROW, C], F32, name="gate_turned", tag="bank7")
@@ -183,7 +184,7 @@ def tile_moe_nxt_lin_none_kernel(tc, xT, w_words, w_scales, wp, gate, offs, out)
             wp_groups[g, a] = keep.tile([P, (b - a) * P * PACK], BF16, name=label, align_bytes=64)
             share = (b - a) * P // len(copies)
             for i, copy in enumerate(copies):
-                interleave(copy, wp_groups[g, a][:], wp_raw[g, a], i * share, (i + 1) * share)
+                interleave(copy, wp_groups[g, a][:], wp_raw[g, a - a % 2][:, :, a % 2 * P :], i * share, (i + 1) * share)
 
         def quantise_wp(g, a, b, buffer=None):
             codes = keep.tile([P, (b - a) * P], U32, name=f"wp_codes{g}{a}", align_bytes=64)
@@ -247,22 +248,26 @@ def tile_moe_nxt_lin_none_kernel(tc, xT, w_words, w_scales, wp, gate, offs, out)
         quantise_wp(0, 0, 2)
         for e in range(4):
             turn(e, 4 + e % 2, scalar)
-            gated_product(e + 2, (2 * (e % 2), 2 * (e % 2) + 1), on_vector=(1,))
+            gated_product(e + 2, (2 * (e % 2), 2 * (e % 2) + 1), on_vector=(1,) if e < 3 else ())
+            if e == 1:
+                group_wp(0, 2, 4, vector)
             quantise_c(e)
-        group_wp(0, 2, 4, vector)
-        quantise_wp(0, 2, 4)
-        group_wp(1, 0, 2, vector)
-        group_wp(1, 2, 4, scalar)
-        quantise_wp(1, 0, 2)
+            if e == 1:
+                quantise_wp(0, 2, 4, buffer="c_group1")
+        group_wp(1, 0, 1, vector)
+        group_wp(1, 1, 2, vector)
+        group_wp(1, 2, 4, vector, scalar)
+        quantise_wp(1, 0, 1)
+        quantise_wp(1, 1, 2)
         quantise_wp(1, 2, 4)
         turn(4, 4, scalar, offset=0)
         turn(5, 5, scalar, offset=2 * N)
-        early = [project(bank, (f, 0, 3)) for f, bank in ((0, 6), (2, 0), (1, 7), (3, 1))]
-        quantise_c(4)
+        early = [project(bank, (f, 0, 3)) for f, bank in ((0, 6), (1, 7), (2, 0), (3, 1))]
         land(vector, early[0])
-        land(vector, early[2])
+        quantise_c(4)
+        land(vector, early[1])
         quantise_c(5)
-        land(scalar, early[1])
+        land(scalar, early[2])
         land(scalar, early[3])
         scatter(True, 0, 0, 3)
         scatter(False, 2, 0, 3)
@@ -270,7 +275,7 @@ def tile_moe_nxt_lin_none_kernel(tc, xT, w_words, w_scales, wp, gate, offs, out)
         land(scalar, project(3, (2, 3, 5)))
         scatter(True, 1, 0, 3)
         scatter(False, 3, 0, 3)
-        land(vector, project(4, (1, 3, E)))
+        land(scalar, project(4, (1, 3, E)))
         land(scalar, project(5, (3, 3, E)))
         scatter(False, 2, 3, 5)
         scatter(True, 0, 3, E)

@@ -91,7 +91,7 @@ def tile_moe_nxt_lin_none_kernel(tc, xT, w_words, w_scales, wp, gate, offs, out)
         wp_raw = {}
 
         def load_wp(g, a, b):
-            if g == 0:
+            if (g, a) != (1, 2):
                 raw = keep.tile([P, PACK, (b - a) * P], F32, name=f"wp_raw{g}{a}", align_bytes=64)
             else:
                 raw = reuse.tile([P, PACK, (b - a) * P], F32, name=f"wp_raw{g}{a}", align_bytes=64, offset=0)
@@ -106,8 +106,9 @@ def tile_moe_nxt_lin_none_kernel(tc, xT, w_words, w_scales, wp, gate, offs, out)
         load_w(2, 4)
         load_scales(1)
         load_wp(0, 2, 4)
+        load_wp(1, 0, 2)
         load_w(4, E)
-        load_wp(1, 0, 4)
+        load_wp(1, 2, 4)
 
         gate_turned = psum.tile([P, PER_ROW, C], F32, name="gate_turned", tag="bank7")
         for c in range(PER_ROW):
@@ -193,7 +194,7 @@ def tile_moe_nxt_lin_none_kernel(tc, xT, w_words, w_scales, wp, gate, offs, out)
             for f in range(a, b):
                 wp_quant[f, g] = (codes[:, (f - a) * P : (f - a + 1) * P], scales[:, (f - a) * P : (f - a + 1) * P])
 
-        windows = [keep.tile([P, T], F32, name=f"window{f}") for f in range(F_TILES)]
+        windows = {f: keep.tile([P, T], F32, name=f"window{f}") for f in (1, 2, 3)}
 
         def project(bank, *parts):
             sums = psum.tile([P, 512], F32, name=f"sums{parts[0][0]}{parts[0][1]}", tag=f"bank{bank}")
@@ -254,28 +255,29 @@ def tile_moe_nxt_lin_none_kernel(tc, xT, w_words, w_scales, wp, gate, offs, out)
             quantise_c(e)
             if e == 1:
                 quantise_wp(0, 2, 4, buffer="c_group1")
-        group_wp(1, 0, 1, vector)
-        group_wp(1, 1, 2, vector)
+                group_wp(1, 0, 2, vector)
+            if e == 2:
+                quantise_wp(1, 0, 2, buffer="c_group2")
         group_wp(1, 2, 4, vector, scalar)
-        quantise_wp(1, 0, 1)
-        quantise_wp(1, 1, 2)
+        early = [project(bank, (f, 0, 3)) for f, bank in ((0, 0), (1, 1))]
+        land(vector, early[0])
         quantise_wp(1, 2, 4)
         turn(4, 4, scalar, offset=0)
         turn(5, 5, scalar, offset=2 * N)
-        early = [project(bank, (f, 0, 3)) for f, bank in ((0, 6), (1, 7), (2, 0), (3, 1))]
-        land(vector, early[0])
-        quantise_c(4)
+        early.extend(project(bank, (f, 0, 3)) for f, bank in ((2, 2), (3, 3)))
         land(vector, early[1])
+        quantise_c(4)
         quantise_c(5)
         land(scalar, early[2])
         land(scalar, early[3])
+        windows[0] = reuse.tile([P, T], F32, name="window0", align_bytes=64, offset=0)
         scatter(True, 0, 0, 3)
         scatter(False, 2, 0, 3)
-        land(vector, project(2, (0, 3, E), (2, 5, E)))
-        land(scalar, project(3, (2, 3, 5)))
+        land(vector, project(6, (0, 3, E), (2, 5, E)))
+        land(scalar, project(7, (2, 3, 5)))
         scatter(True, 1, 0, 3)
         scatter(False, 3, 0, 3)
-        land(scalar, project(4, (1, 3, E)))
+        land(vector, project(4, (1, 3, E)))
         land(scalar, project(5, (3, 3, E)))
         scatter(False, 2, 3, 5)
         scatter(True, 0, 3, E)

@@ -11,7 +11,7 @@ PASSES = N // PASS
 F_TILES = M // P
 GATE_ROWS = 2
 PER_ROW = E // GATE_ROWS
-SCALE_GROUPS = ((0, 2), (2, E))
+SCALE_GROUPS = ((0, 3), (3, E))
 X_CHUNKS = ((0, 512, 208), (512, T, 128))
 
 FLOPS = 2 * K * N * E * C + 2 * N * M * T
@@ -26,6 +26,7 @@ U8 = mybir.dt.uint8
 FP8X4 = mybir.dt.float8_e4m3fn_x4
 FP4X4 = mybir.dt.float4_e2m1fn_x4
 MULT = mybir.AluOpType.mult
+ADD = mybir.AluOpType.add
 COPY = mybir.ActivationFunctionType.Copy
 
 
@@ -40,8 +41,18 @@ def tile_moe_nxt_lin_none_kernel(tc, xT, w_words, w_scales, wp, gate, offs, out)
     nc = tc.nc
     with ExitStack() as ctx:
         keep = ctx.enter_context(tc.tile_pool(name="keep", bufs=1))
-        reuse = ctx.enter_context(tc.tile_pool(name="reuse", bufs=1))
+        shared = ctx.enter_context(tc.tile_pool(name="shared", bufs=1))
         psum = ctx.enter_context(tc.psum_pool(name="psum", bufs=1))
+
+        places = {"end": 0}
+
+        def placed(shape, dtype, name, size, over=None):
+            if over is None:
+                places[name] = places["end"]
+                places["end"] = places["end"] + size
+            else:
+                places[name] = places[over[0]] + over[1]
+            return shared.tile(shape, dtype, name=name, align_bytes=64, offset=places[name])
 
         offsets = keep.tile([P, E * C // 16], U16, name="offsets")
         gate_cols = keep.tile([P, PER_ROW, GATE_ROWS], F32, name="gate_cols")
@@ -73,7 +84,7 @@ def tile_moe_nxt_lin_none_kernel(tc, xT, w_words, w_scales, wp, gate, offs, out)
         w_codes = {}
 
         def load_w(a, b):
-            words = keep.tile([P, b - a, 2 * N], U8, name=f"w_codes{a}", align_bytes=64)
+            words = placed([P, b - a, 2 * N], U8, f"w_codes{a}", (b - a) * 2 * N)
             nc.sync.dma_start(out=words[:].bitcast(I32), in_=w_words[a:b, 0].rearrange("e p n -> p e n").bitcast(I32))
             for e in range(a, b):
                 w_codes[e] = words[:, e - a, :]
@@ -91,10 +102,7 @@ def tile_moe_nxt_lin_none_kernel(tc, xT, w_words, w_scales, wp, gate, offs, out)
         wp_raw = {}
 
         def load_wp(g, a, b):
-            if (g, a) != (1, 2):
-                raw = keep.tile([P, PACK, (b - a) * P], F32, name=f"wp_raw{g}{a}", align_bytes=64)
-            else:
-                raw = reuse.tile([P, PACK, (b - a) * P], F32, name=f"wp_raw{g}{a}", align_bytes=64, offset=0)
+            raw = placed([P, PACK, (b - a) * P], F32, f"wp_raw{g}{a}", 4 * PACK * (b - a) * P)
             nc.sync.dma_start(out=raw[:], in_=wp_view[g][:, :, a * P : b * P])
             for f in range(a, b, 2):
                 wp_raw[g, f] = raw[:, :, (f - a) * P : (f - a + 2) * P]
@@ -102,18 +110,13 @@ def tile_moe_nxt_lin_none_kernel(tc, xT, w_words, w_scales, wp, gate, offs, out)
         load_wp(0, 0, 2)
         load_w(0, 1)
         load_scales(0)
-        load_w(1, 2)
-        load_w(2, 4)
+        load_w(1, 3)
         load_scales(1)
-        load_wp(0, 2, 4)
+        load_w(3, 5)
+        load_w(5, E)
         load_wp(1, 0, 2)
-        load_w(4, E)
+        load_wp(0, 2, 4)
         load_wp(1, 2, 4)
-
-        gate_turned = psum.tile([P, PER_ROW, C], F32, name="gate_turned", tag="bank7")
-        for c in range(PER_ROW):
-            nc.tensor.transpose(gate_turned[:, c, :], gate_rows[:, c * C : (c + 1) * C], ident[:])
-        nc.scalar.copy(out=gate_cols[:], in_=gate_turned[:, :, 0:GATE_ROWS])
 
         x_group = keep.tile([P, PACK * T], BF16, name="x_group", align_bytes=64)
         for (a, b, share), raw in zip(X_CHUNKS, x_raw):
@@ -122,7 +125,13 @@ def tile_moe_nxt_lin_none_kernel(tc, xT, w_words, w_scales, wp, gate, offs, out)
             interleave(nc.vector.tensor_copy, dst, raw, share, b - a)
             nc.vector.quantize_mx(out=x_codes[:, a:b].bitcast(FP8X4), scales=x_scales[:, a:b], in_=dst)
 
-        s_codes, s_scales, rows, c_groups, c_quant, wp_groups, wp_quant = {}, {}, {}, {}, {}, {}, {}
+        gate_turned = psum.tile([P, PER_ROW, C], F32, name="gate_turned", tag="bank7")
+        for c in range(PER_ROW):
+            nc.tensor.transpose(gate_turned[:, c, :], gate_rows[:, c * C : (c + 1) * C], ident[:])
+        nc.scalar.copy(out=gate_cols[:], in_=gate_turned[:, :, 0:GATE_ROWS])
+
+        s_codes, s_scales, ys, rows, turned, c_groups, c_quant = {}, {}, {}, {}, {}, {}, {}
+        wp_groups, wp_quant, landed = {}, {}, {}
 
         def slots(a, b):
             return offsets[:, a * C // 16 : b * C // 16]
@@ -136,12 +145,11 @@ def tile_moe_nxt_lin_none_kernel(tc, xT, w_words, w_scales, wp, gate, offs, out)
                 s_codes[e] = codes[:, (e - a) * C : (e - a + 1) * C]
                 s_scales[e] = scales[:, (e - a) * C : (e - a + 1) * C]
 
-        def gated_product(e, banks, on_vector=()):
+        def product(e, banks):
             for g in range(PASSES):
-                rows[e, g] = keep.tile([P, PASS], BF16, name=f"c_rows{e}{g}", align_bytes=64)
-                y = psum.tile([P, PASS], F32, name=f"y{e}{g}", tag=f"bank{banks[g]}")
+                ys[e, g] = psum.tile([P, PASS], F32, name=f"y{e}{g}", tag=f"bank{banks[g]}")
                 nc.tensor.matmul_mx(
-                    out=y[:],
+                    out=ys[e, g][:],
                     lhsT=s_codes[e].bitcast(FP8X4),
                     lhsT_scale=s_scales[e],
                     rhs=w_codes[e][:, 2 * PASS * g : 2 * PASS * (g + 1)].bitcast(FP4X4),
@@ -149,30 +157,32 @@ def tile_moe_nxt_lin_none_kernel(tc, xT, w_words, w_scales, wp, gate, offs, out)
                     start=True,
                     stop=True,
                 )
-                rounded = rows[e, g][:].rearrange("s (u p i) -> s u p i", u=2, i=2)
-                sums = y[:].rearrange("s (p u i) -> s u p i", u=2, i=2)
-                weight = gate_cols[:, e % PER_ROW, e // PER_ROW : e // PER_ROW + 1]
-                if g in on_vector:
-                    nc.vector.tensor_scalar(out=rounded, in0=sums, scalar1=weight, scalar2=None, op0=MULT)
-                else:
-                    nc.scalar.activation(out=rounded, in_=sums, func=COPY, scale=weight)
 
-        def turn(e, bank, copy, offset=None):
-            turned = psum.tile([P, PASSES, 2, C], F32, name=f"turned{e}", tag=f"bank{bank}")
+        def gated(e, g, on_vector, over=None):
+            rows[e, g] = placed([P, PASS], BF16, f"c_rows{e}{g}", 2 * PASS, over)
+            rounded = rows[e, g][:].rearrange("s (u p i) -> s u p i", u=2, i=2)
+            sums = ys[e, g][:].rearrange("s (p u i) -> s u p i", u=2, i=2)
+            weight = gate_cols[:, e % PER_ROW, e // PER_ROW : e // PER_ROW + 1]
+            if on_vector:
+                nc.vector.tensor_scalar(out=rounded, in0=sums, scalar1=weight, scalar2=None, op0=MULT)
+            else:
+                nc.scalar.activation(out=rounded, in_=sums, func=COPY, scale=weight)
+
+        def turn(e, bank):
+            turned[e] = psum.tile([P, PASSES, 2, C], F32, name=f"turned{e}", tag=f"bank{bank}")
             for g in range(PASSES):
                 words = rows[e, g][:].bitcast(F32)
                 for u in range(2):
-                    nc.tensor.transpose(turned[:, g, u, :], words[:, P * u : P * (u + 1)], ident[:])
-            if offset is None:
-                c_groups[e] = keep.tile([P, N], BF16, name=f"c_group{e}", align_bytes=64)
-            else:
-                c_groups[e] = reuse.tile([P, N], BF16, name=f"c_group{e}", align_bytes=64, offset=offset)
-            pairs = c_groups[e][:].bitcast(F32).rearrange("p (g s u) -> p g s u", g=PASSES, u=2)
-            copy(out=pairs, in_=turned[:].rearrange("p g u s -> p g s u"))
+                    nc.tensor.transpose(turned[e][:, g, u, :], words[:, P * u : P * (u + 1)], ident[:])
 
-        def quantise_c(a, buffer=None):
-            codes = keep.tile([P, 1, PASSES, C], U32, name=f"c_codes{a}", align_bytes=64)
-            scales = keep.tile([P, 1, PASSES, C], U8, name=f"c_scales{a}", tag=buffer or f"c_scales{a}", align_bytes=64)
+        def group_c(e, copy, over=None):
+            c_groups[e] = placed([P, N], BF16, f"c_group{e}", 2 * N, over)
+            pairs = c_groups[e][:].bitcast(F32).rearrange("p (g s u) -> p g s u", g=PASSES, u=2)
+            copy(out=pairs, in_=turned[e][:].rearrange("p g u s -> p g s u"))
+
+        def quantise_c(a, over=None, scales_over=None):
+            codes = placed([P, 1, PASSES, C], U32, f"c_codes{a}", 4 * PASS, over)
+            scales = placed([P, 1, PASSES, C], U8, f"c_scales{a}", PASSES * C, scales_over)
             nc.vector.quantize_mx(
                 out=codes[:].rearrange("p e g s -> p (e g s)").bitcast(FP8X4),
                 scales=scales[:].rearrange("p e g s -> p (e g s)"),
@@ -180,107 +190,146 @@ def tile_moe_nxt_lin_none_kernel(tc, xT, w_words, w_scales, wp, gate, offs, out)
             )
             c_quant[a] = (codes[:, 0], scales[:, 0])
 
-        def group_wp(g, a, b, *copies):
+        def group_wp(g, a, b, *copies, over=None):
             label = f"wp_group{g}{a}"
-            wp_groups[g, a] = keep.tile([P, (b - a) * P * PACK], BF16, name=label, align_bytes=64)
+            wp_groups[g, a] = placed([P, (b - a) * P * PACK], BF16, label, 2 * (b - a) * P * PACK, over)
             share = (b - a) * P // len(copies)
             for i, copy in enumerate(copies):
                 interleave(copy, wp_groups[g, a][:], wp_raw[g, a - a % 2][:, :, a % 2 * P :], i * share, (i + 1) * share)
 
-        def quantise_wp(g, a, b, buffer=None):
+        def quantise_wp(g, a, b, over=None):
             codes = keep.tile([P, (b - a) * P], U32, name=f"wp_codes{g}{a}", align_bytes=64)
-            scales = keep.tile([P, (b - a) * P], U8, name=f"wp_scales{g}{a}", tag=buffer or f"wp_scales{g}{a}", align_bytes=64)
+            scales = placed([P, (b - a) * P], U8, f"wp_scales{g}{a}", (b - a) * P, over)
             nc.vector.quantize_mx(out=codes[:].bitcast(FP8X4), scales=scales[:], in_=wp_groups[g, a][:])
             for f in range(a, b):
                 wp_quant[f, g] = (codes[:, (f - a) * P : (f - a + 1) * P], scales[:, (f - a) * P : (f - a + 1) * P])
 
-        windows = {f: keep.tile([P, T], F32, name=f"window{f}") for f in (1, 2, 3)}
+        windows = {f: keep.tile([P, T], F32, name=f"window{f}") for f in range(F_TILES)}
 
-        def project(bank, *parts):
+        def sums_of(bank, *parts):
             sums = psum.tile([P, 512], F32, name=f"sums{parts[0][0]}{parts[0][1]}", tag=f"bank{bank}")
             steps, col = [], 0
             for f, a, b in parts:
                 steps.extend((f, e, col + (e - a) * C) for e in reversed(range(a, b)))
                 col += (b - a) * C
-            for g in range(PASSES):
-                for i, (f, e, first) in enumerate(steps):
-                    nc.tensor.matmul_mx(
-                        out=sums[:, first : first + C],
-                        lhsT=wp_quant[f, g][0].bitcast(FP8X4),
-                        lhsT_scale=wp_quant[f, g][1],
-                        rhs=c_quant[e][0][:, g, :].bitcast(FP8X4),
-                        rhs_scale=c_quant[e][1][:, g, :],
-                        start=(g == 0 and i == 0),
-                        stop=(g == PASSES - 1 and i == len(steps) - 1),
-                    )
-            return sums, steps
+            return sums, steps, []
 
-        def land(copy, sums, offset=None):
-            bank, places = sums
-            label = "landed%d%d" % places[0][:2]
-            if offset is None:
-                tile = keep.tile([P, len(places) * C], F32, name=label, align_bytes=64)
-            else:
-                tile = reuse.tile([P, len(places) * C], F32, name=label, align_bytes=64, offset=offset)
-            copy(out=tile[:], in_=bank[:, : len(places) * C])
-            for f, e, first in places:
+        def add(sums, passes=range(PASSES), experts=range(E)):
+            bank, steps, done = sums
+            for g in passes:
+                for f, e, first in steps:
+                    if e in experts:
+                        done.append((g, f, e))
+                        nc.tensor.matmul_mx(
+                            out=bank[:, first : first + C],
+                            lhsT=wp_quant[f, g][0].bitcast(FP8X4),
+                            lhsT_scale=wp_quant[f, g][1],
+                            rhs=c_quant[e][0][:, g, :].bitcast(FP8X4),
+                            rhs_scale=c_quant[e][1][:, g, :],
+                            start=len(done) == 1,
+                            stop=len(done) == PASSES * len(steps),
+                        )
+
+        def project(bank, *parts):
+            sums = sums_of(bank, *parts)
+            add(sums)
+            return sums
+
+        def land(copy, sums, over=None):
+            bank, steps, done = sums
+            label = "landed%d%d" % steps[0][:2]
+            tile = placed([P, len(steps) * C], F32, label, 4 * len(steps) * C, over)
+            copy(out=tile[:], in_=bank[:, : len(steps) * C])
+            for f, e, first in steps:
                 landed[f, e] = (tile, first)
 
-        def scatter(on_vector, f, a, b):
+        def scatter(on_vector, f, a, b, store=None):
             tile, first = landed[f, a]
             values = tile[:, first : first + (b - a) * C]
             if on_vector:
                 nc.vector.tensor_copy(windows[f][:].indirect(slots(a, b)), values)
             else:
                 nc.scalar.activation(out=windows[f][:].indirect(slots(a, b)), in_=values, func=COPY)
-            if b == E:
-                queue = nc.sync if on_vector else nc.scalar
-                queue.dma_start(out=out[f * P : (f + 1) * P, :], in_=windows[f][:])
+            if store is not None:
+                store.dma_start(out=out[f * P : (f + 1) * P, :], in_=windows[f][:])
 
-        landed = {}
+        def gpsimd(out, in_):
+            nc.gpsimd.tensor_scalar(out=out, in0=in_, scalar1=1.0, scalar2=0.0, op0=MULT, op1=ADD)
+
         vector, scalar = nc.vector.tensor_copy, nc.scalar.copy
 
         group_wp(0, 0, 2, scalar)
         gather(0, 1)
-        gated_product(0, (0, 1))
+        product(0, (0, 1))
         gather(1, 3)
+        product(1, (2, 3))
+        product(2, (6, 7))
         gather(3, E)
-        gated_product(1, (2, 3))
+        gated(0, 0, False)
+        gated(0, 1, False)
+        gated(1, 0, False)
+        gated(1, 1, True)
+        turn(0, 2)
+        turn(1, 5)
         quantise_wp(0, 0, 2)
-        for e in range(4):
-            turn(e, 4 + e % 2, scalar)
-            gated_product(e + 2, (2 * (e % 2), 2 * (e % 2) + 1), on_vector=(1,) if e < 3 else ())
-            if e == 1:
-                group_wp(0, 2, 4, vector)
-            quantise_c(e)
-            if e == 1:
-                quantise_wp(0, 2, 4, buffer="c_group1")
-                group_wp(1, 0, 2, vector)
-            if e == 2:
-                quantise_wp(1, 0, 2, buffer="c_group2")
-        group_wp(1, 2, 4, vector, scalar)
-        early = [project(bank, (f, 0, 3)) for f, bank in ((0, 0), (1, 1))]
-        land(vector, early[0])
-        quantise_wp(1, 2, 4)
-        turn(4, 4, scalar, offset=0)
-        turn(5, 5, scalar, offset=2 * N)
-        early.extend(project(bank, (f, 0, 3)) for f, bank in ((2, 2), (3, 3)))
-        land(vector, early[1])
+        gated(2, 0, False)
+        gated(2, 1, True)
+        product(3, (0, 1))
+        product(4, (4, 3))
+        product(5, (6, 7))
+        group_c(0, scalar)
+        group_c(1, scalar)
+        quantise_c(0)
+        gated(3, 0, False)
+        gated(3, 1, True)
+        turn(2, 0)
+        turn(3, 2)
+        quantise_c(1, scales_over=("w_codes3", 0))
+        gated(4, 0, False)
+        gated(4, 1, True)
+        turn(4, 5)
+        gated(5, 0, False)
+        group_c(2, scalar)
+        group_wp(1, 0, 2, vector)
+        quantise_c(2)
+        quantise_wp(1, 0, 2)
+        lower = [project(1, (0, 0, 2), (1, 0, 2))]
+        group_c(3, scalar)
+        gated(5, 1, False)
+        turn(5, 0)
+        group_wp(0, 2, 4, vector)
+        quantise_c(3)
+        group_c(4, scalar)
+        quantise_wp(0, 2, 4)
+        upper = sums_of(4, (2, 0, 2), (3, 0, 2))
+        add(upper, passes=(0,))
+        late = {f: sums_of(bank, (f, 2, E)) for f, bank in ((0, 3), (2, 6), (1, 7), (3, 2))}
+        for f in (0, 1):
+            add(late[f], experts=(2, 3))
+        land(scalar, lower[0])
+        group_c(5, scalar)
+        group_wp(1, 2, 4, vector)
         quantise_c(4)
+        quantise_wp(1, 2, 4)
+        add(upper, passes=(1,))
         quantise_c(5)
-        land(scalar, early[2])
-        land(scalar, early[3])
-        windows[0] = reuse.tile([P, T], F32, name="window0", align_bytes=64, offset=0)
-        scatter(True, 0, 0, 3)
-        scatter(False, 2, 0, 3)
-        land(vector, project(6, (0, 3, E), (2, 5, E)))
-        land(scalar, project(7, (2, 3, 5)))
-        scatter(True, 1, 0, 3)
-        scatter(False, 3, 0, 3)
-        land(vector, project(4, (1, 3, E)))
-        land(scalar, project(5, (3, 3, E)))
-        scatter(False, 2, 3, 5)
-        scatter(True, 0, 3, E)
-        scatter(True, 2, 5, E)
-        scatter(True, 1, 3, E)
-        scatter(False, 3, 3, E)
+        for f in (2, 3):
+            add(late[f], experts=(2, 3))
+        for e in (4, 5):
+            for f in (1, 3, 0, 2):
+                add(late[f], experts=(e,))
+        scatter(False, 0, 0, 2)
+        scatter(True, 1, 0, 2)
+        land(scalar, upper)
+        scatter(False, 2, 0, 2)
+        scatter(True, 3, 0, 2)
+        land(scalar, late[0], over=("c_codes5", 0))
+        land(scalar, late[2])
+        land(vector, late[1])
+        land(vector, late[3])
+        scatter(False, 0, 2, 4)
+        scatter(True, 1, 2, E, store=nc.sync)
+        scatter(False, 2, 2, 4)
+        scatter(False, 0, 4, E, store=nc.scalar)
+        scatter(True, 3, 2, E, store=nc.sync)
+        scatter(False, 2, 4, E, store=nc.scalar)

@@ -107,13 +107,13 @@ def tile_moe_nxt_lin_none_kernel(tc, xT, w_words, w_scales, wp, gate, offs, out)
             for f in range(a, b, 2):
                 wp_raw[g, f] = raw[:, :, (f - a) * P : (f - a + 2) * P]
 
-        load_wp(0, 0, 2)
         load_w(0, 1)
         load_scales(0)
         load_w(1, 3)
         load_scales(1)
         load_w(3, 5)
         load_w(5, E)
+        load_wp(0, 0, 2)
         load_wp(1, 0, 2)
         load_wp(0, 2, 4)
         load_wp(1, 2, 4)
@@ -243,22 +243,22 @@ def tile_moe_nxt_lin_none_kernel(tc, xT, w_words, w_scales, wp, gate, offs, out)
             for f, e, first in steps:
                 landed[f, e] = (tile, first)
 
-        def scatter(on_vector, f, a, b, store=None):
+        def scatter(on_vector, f, a, b):
             tile, first = landed[f, a]
             values = tile[:, first : first + (b - a) * C]
             if on_vector:
                 nc.vector.tensor_copy(windows[f][:].indirect(slots(a, b)), values)
             else:
                 nc.scalar.activation(out=windows[f][:].indirect(slots(a, b)), in_=values, func=COPY)
-            if store is not None:
-                store.dma_start(out=out[f * P : (f + 1) * P, :], in_=windows[f][:])
+
+        def store(queue, f):
+            queue.dma_start(out=out[f * P : (f + 1) * P, :], in_=windows[f][:])
 
         def gpsimd(out, in_):
             nc.gpsimd.tensor_scalar(out=out, in0=in_, scalar1=1.0, scalar2=0.0, op0=MULT, op1=ADD)
 
         vector, scalar = nc.vector.tensor_copy, nc.scalar.copy
 
-        group_wp(0, 0, 2, scalar)
         gather(0, 1)
         product(0, (0, 1))
         gather(1, 3)
@@ -269,54 +269,45 @@ def tile_moe_nxt_lin_none_kernel(tc, xT, w_words, w_scales, wp, gate, offs, out)
         gated(0, 1, False)
         gated(1, 0, False)
         gated(1, 1, True)
-        turn(0, 2)
-        turn(1, 5)
-        quantise_wp(0, 0, 2)
+        product(3, (0, 1))
         gated(2, 0, False)
         gated(2, 1, True)
-        product(3, (0, 1))
-        product(4, (4, 3))
+        product(4, (2, 3))
         product(5, (6, 7))
+        for e in range(3, E):
+            gated(e, 0, False)
+            gated(e, 1, e < 5)
+        for e, bank in enumerate((0, 1, 2, 4, 5, 3)):
+            turn(e, bank)
+        group_wp(0, 0, 2, vector)
+        quantise_wp(0, 0, 2)
+        group_wp(1, 0, 2, vector)
         group_c(0, scalar)
         group_c(1, scalar)
         quantise_c(0)
-        gated(3, 0, False)
-        gated(3, 1, True)
-        turn(2, 0)
-        turn(3, 2)
-        quantise_c(1, scales_over=("w_codes3", 0))
-        gated(4, 0, False)
-        gated(4, 1, True)
-        turn(4, 5)
-        gated(5, 0, False)
-        group_c(2, scalar)
-        group_wp(1, 0, 2, vector)
-        quantise_c(2)
         quantise_wp(1, 0, 2)
-        lower = [project(1, (0, 0, 2), (1, 0, 2))]
-        group_c(3, scalar)
-        gated(5, 1, False)
-        turn(5, 0)
+        quantise_c(1)
+        lower = sums_of(6, (0, 0, 2), (1, 0, 2))
+        for e in range(2):
+            add(lower, experts=(e,))
+        for e in range(2, 5):
+            group_c(e, scalar)
         group_wp(0, 2, 4, vector)
-        quantise_c(3)
-        group_c(4, scalar)
+        quantise_c(2)
         quantise_wp(0, 2, 4)
-        upper = sums_of(4, (2, 0, 2), (3, 0, 2))
+        upper = sums_of(7, (2, 0, 2), (3, 0, 2))
         add(upper, passes=(0,))
-        late = {f: sums_of(bank, (f, 2, E)) for f, bank in ((0, 3), (2, 6), (1, 7), (3, 2))}
-        for f in (0, 1):
-            add(late[f], experts=(2, 3))
-        land(scalar, lower[0])
+        land(scalar, lower)
         group_c(5, scalar)
         group_wp(1, 2, 4, vector)
-        quantise_c(4)
+        quantise_c(3)
         quantise_wp(1, 2, 4)
         add(upper, passes=(1,))
+        late = {f: sums_of(bank, (f, 2, E)) for f, bank in ((0, 0), (2, 1), (1, 2), (3, 4))}
+        quantise_c(4)
         quantise_c(5)
-        for f in (2, 3):
-            add(late[f], experts=(2, 3))
-        for e in (4, 5):
-            for f in (1, 3, 0, 2):
+        for e in range(2, E):
+            for f in (1, 0, 2, 3):
                 add(late[f], experts=(e,))
         scatter(False, 0, 0, 2)
         scatter(True, 1, 0, 2)
@@ -325,11 +316,15 @@ def tile_moe_nxt_lin_none_kernel(tc, xT, w_words, w_scales, wp, gate, offs, out)
         scatter(True, 3, 0, 2)
         land(scalar, late[0], over=("c_codes5", 0))
         land(scalar, late[2])
+        land(scalar, late[3])
         land(vector, late[1])
-        land(vector, late[3])
         scatter(False, 0, 2, 4)
-        scatter(True, 1, 2, E, store=nc.sync)
+        scatter(True, 1, 2, E)
+        store(nc.sync, 1)
         scatter(False, 2, 2, 4)
-        scatter(False, 0, 4, E, store=nc.scalar)
-        scatter(True, 3, 2, E, store=nc.sync)
-        scatter(False, 2, 4, E, store=nc.scalar)
+        scatter(False, 0, 4, E)
+        scatter(True, 3, 2, E)
+        store(nc.sync, 3)
+        scatter(False, 2, 4, E)
+        store(nc.scalar, 0)
+        store(nc.scalar, 2)

from contextlib import ExitStack

import concourse.mybir as mybir
from concourse.masks import make_identity

K, T, E, C, N, M = 512, 768, 6, 128, 1024, 512
P = 128
PACK = 4
PASS = P * PACK
PASSES = N // PASS
F_TILES = M // P
GATE_ROWS = 2
PER_ROW = E // GATE_ROWS
SCALE_GROUPS = ((0, 3), (3, E))
X_CHUNKS = ((0, 512, 208), (512, T, 128))

FLOPS = 2 * K * N * E * C + 2 * N * M * T
BYTES = 4 * K * T + E * K * N // 2 + E * (K // 32) * N + 4 * N * M + 4 * E * C + 2 * E * C + 4 * M * T

F32 = mybir.dt.float32
BF16 = mybir.dt.bfloat16
I32 = mybir.dt.int32
U32 = mybir.dt.uint32
U16 = mybir.dt.uint16
U8 = mybir.dt.uint8
FP8X4 = mybir.dt.float8_e4m3fn_x4
FP4X4 = mybir.dt.float4_e2m1fn_x4
MULT = mybir.AluOpType.mult
ADD = mybir.AluOpType.add
COPY = mybir.ActivationFunctionType.Copy


def interleave(copy, dst, src, a, b):
    copy(
        out=dst[:, PACK * a : PACK * b].rearrange("p (c i j) -> p c j i", i=4, j=PACK),
        in_=src[:, :, a:b].rearrange("p j (c i) -> p c j i", i=4),
    )


def tile_moe_nxt_lin_none_kernel(tc, xT, w_words, w_scales, wp, gate, offs, out):
    nc = tc.nc
    with ExitStack() as ctx:
        keep = ctx.enter_context(tc.tile_pool(name="keep", bufs=1))
        shared = ctx.enter_context(tc.tile_pool(name="shared", bufs=1))
        psum = ctx.enter_context(tc.psum_pool(name="psum", bufs=1))

        places = {"end": 0}

        def placed(shape, dtype, name, size, over=None):
            if over is None:
                places[name] = places["end"]
                places["end"] = places["end"] + size
            else:
                places[name] = places[over[0]] + over[1]
            return shared.tile(shape, dtype, name=name, align_bytes=64, offset=places[name])

        offsets = keep.tile([P, E * C // 16], U16, name="offsets")
        gate_cols = keep.tile([P, PER_ROW, GATE_ROWS], F32, name="gate_cols")
        gate_rows = keep.tile([P, PER_ROW * C], F32, name="gate_rows")
        ident = keep.tile([P, P], F32, name="ident")
        x_codes = keep.tile([P, T], U32, name="x_codes", align_bytes=64)
        x_scales = keep.tile([P, T], U8, name="x_scales", align_bytes=64)
        w_scale_tiles = [keep.tile([P, b - a, N], U8, name=f"w_scales{a}", align_bytes=64) for a, b in SCALE_GROUPS]
        w_planes = [tile[:, e, :] for tile, (a, b) in zip(w_scale_tiles, SCALE_GROUPS) for e in range(b - a)]

        nc.gpsimd.memset(gate_rows[:], 0.0)
        for tile in w_scale_tiles:
            nc.vector.memset(tile[:].rearrange("p e n -> p (e n)").bitcast(I32), 0)
        nc.gpsimd.memset(x_scales[:], 0)
        make_identity(nc, ident[:])

        x_view = xT.rearrange("(p j) t -> p j t", j=PACK)
        x_raw = []
        for a, b, share in X_CHUNKS:
            raw = keep.tile([P, PACK, b - a], F32, name=f"x_raw{a}")
            nc.sync.dma_start(out=raw[:], in_=x_view[:, :, a:b])
            x_raw.append(raw)
            if a == 0:
                nc.sync.dma_start(offsets[:], offs)
                nc.sync.dma_start(
                    out=gate_rows[0:GATE_ROWS, :], in_=gate[0:1, :].rearrange("o (r s) -> (o r) s", r=GATE_ROWS)
                )

        w_codes = {}

        def load_w(a, b):
            words = placed([P, b - a, 2 * N], U8, f"w_codes{a}", (b - a) * 2 * N)
            nc.sync.dma_start(out=words[:].bitcast(I32), in_=w_words[a:b, 0].rearrange("e p n -> p e n").bitcast(I32))
            for e in range(a, b):
                w_codes[e] = words[:, e - a, :]

        scale_rows = w_scales.bitcast(I32).rearrange("e a (q r) n -> r q (e a) n", r=4)

        def load_scales(i):
            for r in range(4):
                nc.sync.dma_start(
                    out=w_scale_tiles[i][r:P:32, :, :].bitcast(I32),
                    in_=scale_rows[r, :, SCALE_GROUPS[i][0] : SCALE_GROUPS[i][1], :],
                )

        wp_view = wp.rearrange("(g p j) f -> g p j f", p=P, j=PACK)
        wp_raw = {}

        def load_wp(g, a, b):
            raw = placed([P, PACK, (b - a) * P], F32, f"wp_raw{g}{a}", 4 * PACK * (b - a) * P)
            nc.sync.dma_start(out=raw[:], in_=wp_view[g][:, :, a * P : b * P])
            for f in range(a, b, 2):
                wp_raw[g, f] = raw[:, :, (f - a) * P : (f - a + 2) * P]

        load_w(0, 1)
        load_scales(0)
        load_w(1, 3)
        load_scales(1)
        load_w(3, 5)
        load_w(5, E)
        load_wp(0, 0, 2)
        load_wp(1, 0, 2)
        load_wp(0, 2, 4)
        load_wp(1, 2, 4)

        x_group = keep.tile([P, PACK * T], BF16, name="x_group", align_bytes=64)
        for (a, b, share), raw in zip(X_CHUNKS, x_raw):
            dst = x_group[:, PACK * a : PACK * b]
            interleave(nc.scalar.copy, dst, raw, 0, share)
            interleave(nc.vector.tensor_copy, dst, raw, share, b - a)
            nc.vector.quantize_mx(out=x_codes[:, a:b].bitcast(FP8X4), scales=x_scales[:, a:b], in_=dst)

        gate_turned = psum.tile([P, PER_ROW, C], F32, name="gate_turned", tag="bank7")
        for c in range(PER_ROW):
            nc.tensor.transpose(gate_turned[:, c, :], gate_rows[:, c * C : (c + 1) * C], ident[:])
        nc.scalar.copy(out=gate_cols[:], in_=gate_turned[:, :, 0:GATE_ROWS])

        s_codes, s_scales, ys, rows, turned, c_groups, c_quant = {}, {}, {}, {}, {}, {}, {}
        wp_groups, wp_quant, landed = {}, {}, {}

        def slots(a, b):
            return offsets[:, a * C // 16 : b * C // 16]

        def gather(a, b):
            codes = keep.tile([P, (b - a) * C], U32, name=f"s_codes{a}", align_bytes=64)
            scales = keep.tile([P, (b - a) * C], U8, name=f"s_scales{a}", align_bytes=64)
            nc.vector.tensor_copy(codes[:], x_codes[:].indirect(slots(a, b)))
            nc.vector.tensor_copy(scales[:], x_scales[:].indirect(slots(a, b)))
            for e in range(a, b):
                s_codes[e] = codes[:, (e - a) * C : (e - a + 1) * C]
                s_scales[e] = scales[:, (e - a) * C : (e - a + 1) * C]

        def product(e, banks):
            for g in range(PASSES):
                ys[e, g] = psum.tile([P, PASS], F32, name=f"y{e}{g}", tag=f"bank{banks[g]}")
                nc.tensor.matmul_mx(
                    out=ys[e, g][:],
                    lhsT=s_codes[e].bitcast(FP8X4),
                    lhsT_scale=s_scales[e],
                    rhs=w_codes[e][:, 2 * PASS * g : 2 * PASS * (g + 1)].bitcast(FP4X4),
                    rhs_scale=w_planes[e][:, PASS * g : PASS * (g + 1)],
                    start=True,
                    stop=True,
                )

        def gated(e, g, on_vector, over=None):
            rows[e, g] = placed([P, PASS], BF16, f"c_rows{e}{g}", 2 * PASS, over)
            rounded = rows[e, g][:].rearrange("s (u p i) -> s u p i", u=2, i=2)
            sums = ys[e, g][:].rearrange("s (p u i) -> s u p i", u=2, i=2)
            weight = gate_cols[:, e % PER_ROW, e // PER_ROW : e // PER_ROW + 1]
            if on_vector:
                nc.vector.tensor_scalar(out=rounded, in0=sums, scalar1=weight, scalar2=None, op0=MULT)
            else:
                nc.scalar.activation(out=rounded, in_=sums, func=COPY, scale=weight)

        def turn(e, bank):
            turned[e] = psum.tile([P, PASSES, 2, C], F32, name=f"turned{e}", tag=f"bank{bank}")
            for g in range(PASSES):
                words = rows[e, g][:].bitcast(F32)
                for u in range(2):
                    nc.tensor.transpose(turned[e][:, g, u, :], words[:, P * u : P * (u + 1)], ident[:])

        def group_c(e, copy, over=None):
            c_groups[e] = placed([P, N], BF16, f"c_group{e}", 2 * N, over)
            pairs = c_groups[e][:].bitcast(F32).rearrange("p (g s u) -> p g s u", g=PASSES, u=2)
            copy(out=pairs, in_=turned[e][:].rearrange("p g u s -> p g s u"))

        def quantise_c(a, over=None, scales_over=None):
            codes = placed([P, 1, PASSES, C], U32, f"c_codes{a}", 4 * PASS, over)
            scales = placed([P, 1, PASSES, C], U8, f"c_scales{a}", PASSES * C, scales_over)
            nc.vector.quantize_mx(
                out=codes[:].rearrange("p e g s -> p (e g s)").bitcast(FP8X4),
                scales=scales[:].rearrange("p e g s -> p (e g s)"),
                in_=c_groups[a][:],
            )
            c_quant[a] = (codes[:, 0], scales[:, 0])

        def group_wp(g, a, b, *copies, over=None):
            label = f"wp_group{g}{a}"
            wp_groups[g, a] = placed([P, (b - a) * P * PACK], BF16, label, 2 * (b - a) * P * PACK, over)
            share = (b - a) * P // len(copies)
            for i, copy in enumerate(copies):
                interleave(copy, wp_groups[g, a][:], wp_raw[g, a - a % 2][:, :, a % 2 * P :], i * share, (i + 1) * share)

        def quantise_wp(g, a, b, over=None):
            codes = keep.tile([P, (b - a) * P], U32, name=f"wp_codes{g}{a}", align_bytes=64)
            scales = placed([P, (b - a) * P], U8, f"wp_scales{g}{a}", (b - a) * P, over)
            nc.vector.quantize_mx(out=codes[:].bitcast(FP8X4), scales=scales[:], in_=wp_groups[g, a][:])
            for f in range(a, b):
                wp_quant[f, g] = (codes[:, (f - a) * P : (f - a + 1) * P], scales[:, (f - a) * P : (f - a + 1) * P])

        windows = {f: keep.tile([P, T], F32, name=f"window{f}") for f in range(F_TILES)}

        def sums_of(bank, *parts):
            sums = psum.tile([P, 512], F32, name=f"sums{parts[0][0]}{parts[0][1]}", tag=f"bank{bank}")
            steps, col = [], 0
            for f, a, b in parts:
                steps.extend((f, e, col + (e - a) * C) for e in reversed(range(a, b)))
                col += (b - a) * C
            return sums, steps, []

        def add(sums, passes=range(PASSES), experts=range(E)):
            bank, steps, done = sums
            for g in passes:
                for f, e, first in steps:
                    if e in experts:
                        done.append((g, f, e))
                        nc.tensor.matmul_mx(
                            out=bank[:, first : first + C],
                            lhsT=wp_quant[f, g][0].bitcast(FP8X4),
                            lhsT_scale=wp_quant[f, g][1],
                            rhs=c_quant[e][0][:, g, :].bitcast(FP8X4),
                            rhs_scale=c_quant[e][1][:, g, :],
                            start=len(done) == 1,
                            stop=len(done) == PASSES * len(steps),
                        )

        def project(bank, *parts):
            sums = sums_of(bank, *parts)
            add(sums)
            return sums

        def land(copy, sums, over=None):
            bank, steps, done = sums
            label = "landed%d%d" % steps[0][:2]
            tile = placed([P, len(steps) * C], F32, label, 4 * len(steps) * C, over)
            copy(out=tile[:], in_=bank[:, : len(steps) * C])
            for f, e, first in steps:
                landed[f, e] = (tile, first)

        def scatter(on_vector, f, a, b):
            tile, first = landed[f, a]
            values = tile[:, first : first + (b - a) * C]
            if on_vector:
                nc.vector.tensor_copy(windows[f][:].indirect(slots(a, b)), values)
            else:
                nc.scalar.activation(out=windows[f][:].indirect(slots(a, b)), in_=values, func=COPY)

        def store(queue, f):
            queue.dma_start(out=out[f * P : (f + 1) * P, :], in_=windows[f][:])

        def gpsimd(out, in_):
            nc.gpsimd.tensor_scalar(out=out, in0=in_, scalar1=1.0, scalar2=0.0, op0=MULT, op1=ADD)

        vector, scalar = nc.vector.tensor_copy, nc.scalar.copy

        gather(0, 1)
        product(0, (0, 1))
        gather(1, 3)
        product(1, (2, 3))
        product(2, (6, 7))
        gather(3, E)
        gated(0, 0, False)
        gated(0, 1, False)
        gated(1, 0, False)
        gated(1, 1, True)
        product(3, (0, 1))
        gated(2, 0, False)
        gated(2, 1, True)
        product(4, (2, 3))
        product(5, (6, 7))
        for e in range(3, E):
            gated(e, 0, False)
            gated(e, 1, e < 5)
        for e, bank in enumerate((0, 1, 2, 4, 5, 3)):
            turn(e, bank)
        group_wp(0, 0, 2, vector)
        quantise_wp(0, 0, 2)
        group_wp(1, 0, 2, vector)
        group_c(0, scalar)
        group_c(1, scalar)
        quantise_c(0)
        quantise_wp(1, 0, 2)
        quantise_c(1)
        lower = sums_of(6, (0, 0, 2), (1, 0, 2))
        for e in range(2):
            add(lower, experts=(e,))
        for e in range(2, 5):
            group_c(e, scalar)
        group_wp(0, 2, 4, vector)
        quantise_c(2)
        quantise_wp(0, 2, 4)
        upper = sums_of(7, (2, 0, 2), (3, 0, 2))
        add(upper, passes=(0,))
        land(scalar, lower)
        group_c(5, scalar)
        group_wp(1, 2, 4, vector)
        quantise_c(3)
        quantise_wp(1, 2, 4)
        add(upper, passes=(1,))
        late = {f: sums_of(bank, (f, 2, E)) for f, bank in ((0, 0), (2, 1), (1, 2), (3, 4))}
        quantise_c(4)
        quantise_c(5)
        for e in range(2, E):
            for f in (1, 0, 2, 3):
                add(late[f], experts=(e,))
        scatter(False, 0, 0, 2)
        scatter(True, 1, 0, 2)
        land(scalar, upper)
        scatter(False, 2, 0, 2)
        scatter(True, 3, 0, 2)
        land(scalar, late[0], over=("c_codes5", 0))
        land(scalar, late[2])
        land(scalar, late[3])
        land(vector, late[1])
        scatter(False, 0, 2, 4)
        scatter(True, 1, 2, E)
        store(nc.sync, 1)
        scatter(False, 2, 2, 4)
        scatter(False, 0, 4, E)
        scatter(True, 3, 2, E)
        store(nc.sync, 3)
        scatter(False, 2, 4, E)
        store(nc.scalar, 0)
        store(nc.scalar, 2)
